import numpy as np
import ml_dtypes


def mxq(x, axis, fmt="e4m3"):
    dtype, down = {"e4m3": (ml_dtypes.float8_e4m3fn, 7), "e5m2": (ml_dtypes.float8_e5m2, 14)}[fmt]
    v = np.moveaxis(np.asarray(x, np.float32).astype(ml_dtypes.bfloat16).astype(np.float64), axis, -1)
    blocks = v.reshape(v.shape[:-1] + (-1, 32))
    amax = np.abs(blocks).max(-1, keepdims=True)
    byte = np.maximum(np.where(amax > 0, np.frexp(amax)[1] - 1 + 127, 0) - down, 1)
    scale = np.exp2(byte - 127.0)
    codes = (blocks / scale).astype(np.float32).astype(dtype).astype(np.float64)
    return np.moveaxis((codes * scale).reshape(v.shape), -1, axis)


WIDE = False


def mx_kscale(k):
    if not WIDE:
        return np.ones(k)
    levels = np.array([10, -10, 5, -5, 0])
    if k % 512:
        return np.exp2(np.random.permutation(np.resize(levels, k // 32))).repeat(32)
    a = np.empty((k // 512, 16))
    for p in range(k // 512):
        a[p, :8] = np.random.permutation(np.resize(levels, 8))
        for g in range(8):
            far = levels[np.abs(levels - a[p, g]) >= 10]
            a[p, g + 8] = far[np.random.randint(len(far))]
    return np.exp2(a.ravel()).repeat(32)


BF16 = ml_dtypes.bfloat16


def bf(x):
    return np.asarray(x, np.float32).astype(BF16)


def f64(x):
    return np.asarray(x).astype(np.float64)

def planes(Y):
    n, m = Y.shape
    b = f64(bf(Y)).reshape(n // 32, 32, m)
    amax = np.abs(b).max(1)
    byte = np.clip(np.where(amax > 0, np.frexp(amax)[1] - 1 + 127 - 7, 1), 1, 254)
    codes = (b * np.exp2(127.0 - byte)[:, None, :]).reshape(n, m).astype(np.float32).astype(ml_dtypes.float8_e4m3fn).view(np.uint8)
    words = codes.reshape(n // 512, 128, 4, m).transpose(0, 1, 3, 2)
    return np.ascontiguousarray(words), np.ascontiguousarray(byte.astype(np.uint8).reshape(n // 512, 16, m))


B, T, K, KT, D = 128, 16, 1024, 512, 1024

def setup_inputs():
    s = mx_kscale(K)
    r = mx_kscale(KT)
    spread = np.exp(0.6 * np.random.randn(D))
    patches = np.random.randn(B, T, K)
    w_patch = np.random.randn(K, D) * spread / np.sqrt(K)
    text = np.random.randn(B, KT)
    w_text = 0.6 * np.random.randn(KT, D) * spread / np.sqrt(KT)
    scale = 0.25 * np.random.randn(D, B)
    shift = 0.4 * np.random.randn(D, B) * spread[:, None]
    return {
        "patches": bf(patches * s),
        "w_patch": bf(w_patch / s[:, None]),
        "text": bf(text * r),
        "w_text": bf(w_text / r[:, None]),
        "scale": bf(scale),
        "shift": bf(shift),
    }

def reference(patches, w_patch, text, w_text, scale, shift):
    qp = mxq(f64(patches).reshape(B * T, K), 1, "e4m3")
    qw = mxq(f64(w_patch), 0, "e4m3")
    u = (qw.T @ qp.T).reshape(D, B, T)
    qt = mxq(f64(text), 1, "e4m3")
    qv = mxq(f64(w_text), 0, "e4m3")
    c = qv.T @ qt.T
    y = (1.0 + f64(scale)[:, :, None]) * u + f64(shift)[:, :, None] + c[:, :, None]
    Y = y.reshape(D, B * T)
    words, scales = planes(Y)
    return y, words, scales

@@ -1,0 +1,389 @@
+from contextlib import ExitStack
+
+import concourse.mybir as mybir
+from concourse.masks import make_identity
+
+B, T, K, KT, D = 128, 16, 1024, 512, 1024
+M = B * T
+FLOPS = 2 * D * M * K + 2 * D * B * KT
+
+F32 = mybir.dt.float32
+BF16 = mybir.dt.bfloat16
+I32 = mybir.dt.int32
+U32 = mybir.dt.uint32
+U8 = mybir.dt.uint8
+FP8X4 = mybir.dt.float8_e4m3fn_x4
+ALU = mybir.AluOpType
+ACT = mybir.ActivationFunctionType
+
+P = 128
+PACK = 4
+K_PASS = P * PACK
+PASSES = K // K_PASS
+GROUPS = D // K_PASS
+CHUNK = 512
+CHUNKS = M // CHUNK
+IMAGES = CHUNK // T
+ROW_TILES = CHUNK // P
+PAIR = 2 * P
+UNITS = GROUPS * CHUNKS
+POOL_SLOTS = 2
+HEAD_VECTOR_SLOTS = 3
+TAIL_VECTOR_COLS = 320
+
+
+def tile_patch_modulate_text_planes_g2_kernel(
+    tc, patches, w_patch, text, w_text, scale, shift, out_0, out_1, out_2
+):
+    nc = tc.nc
+    rows = patches.rearrange("b j k -> (b j) k")
+    y_out = out_0.rearrange("d b j -> d (b j)")
+    words_out = out_1.rearrange("g p m t -> g p (m t)").bitcast(I32)
+    scales_out = out_2.bitcast(I32)
+
+    with ExitStack() as ctx:
+        keep = ctx.enter_context(tc.tile_pool(name="keep", bufs=1))
+        stage = ctx.enter_context(tc.tile_pool(name="stage", bufs=2))
+        psum = ctx.enter_context(tc.psum_pool(name="psum", bufs=1))
+        ctx.enter_context(tc.manual_schedule())
+
+        ident = keep.tile([P, P], F32, name="ident")
+        make_identity(nc, ident[:])
+
+        patch_raw, weight_raw, scale_sb, shift_sb = {}, {}, {}, {}
+
+        def load_patches(pair):
+            raw = keep.tile([P, 2, K], BF16, name="patch_raw%d" % pair)
+            src = rows[2 * P * pair : 2 * P * (pair + 1), :]
+            nc.sync.dma_start(out=raw[:], in_=src.rearrange("(n p) k -> p n k", p=P))
+            patch_raw[pair] = raw
+
+        def load_weight(g, h):
+            w = w_text if h == PASSES else w_patch[K_PASS * h : K_PASS * (h + 1), :]
+            raw = keep.tile([P, PACK, K_PASS], BF16, name="weight_raw%d_%d" % (g, h))
+            src = w[:, K_PASS * g : K_PASS * (g + 1)]
+            nc.sync.dma_start(out=raw[:], in_=src.rearrange("(p j) c -> p j c", j=PACK))
+            weight_raw[g, h] = raw
+
+        def load_modulation(g):
+            for name, src, dst in (("scale", scale, scale_sb), ("shift", shift, shift_sb)):
+                sb = keep.tile([P, PACK, B], BF16, name="%s%d" % (name, g))
+                part = src[K_PASS * g : K_PASS * (g + 1), :]
+                nc.sync.dma_start(out=sb[:], in_=part.rearrange("(p t) b -> p t b", t=PACK))
+                dst[g] = sb
+
+        text_raw = keep.tile([P, KT], BF16, name="text_raw")
+        load_weight(0, 0)
+        load_patches(0)
+        load_weight(0, PASSES)
+        nc.sync.dma_start(out=text_raw[:], in_=text)
+        load_weight(0, 1)
+        load_modulation(0)
+        load_weight(1, PASSES)
+        load_patches(1)
+        load_weight(1, 0)
+        load_patches(2)
+        load_weight(1, 1)
+        load_modulation(1)
+        for pair in range(3, 8):
+            load_patches(pair)
+
+        def turn(raw_row, passes, dst_words):
+            bank = psum.tile([P, passes * 2 * P], F32, name="turn", tag="turn", bufs=2)
+            words = raw_row.bitcast(F32)
+            for h in range(passes):
+                for u in range(2):
+                    col = (2 * h + u) * P
+                    nc.tensor.transpose(
+                        bank[:, col : col + P], words[:, 2 * P * h + u : 2 * P * (h + 1) : 2], ident[:]
+                    )
+            nc.scalar.copy(
+                out=dst_words.rearrange("p h (m u) -> p h m u", u=2),
+                in_=bank[:].rearrange("p (h u m) -> p h m u", h=passes, u=2),
+            )
+
+        patch_codes = keep.tile([P, CHUNKS, PASSES, CHUNK], U32, name="patch_codes", align_bytes=64)
+        patch_scales = keep.tile([P, CHUNKS, PASSES, CHUNK], U8, name="patch_scales", align_bytes=64)
+
+        def turn_patch_tile(tile_no, grouped, at):
+            raw = patch_raw[tile_no // 2]
+            turn(raw[:, tile_no % 2, :], PASSES, grouped[:, :, 2 * P * at : 2 * P * (at + 1)])
+
+        def quantize(codes, scales, values):
+            nc.vector.quantize_mx(out=codes.bitcast(FP8X4), scales=scales, in_=values)
+
+        weight_grouped, weight_codes, weight_scales = {}, {}, {}
+
+        def interleave_weight(g, h, vector_slots):
+            grouped = stage.tile([P, PACK, K_PASS], BF16, name="weight_grouped", bufs=4, align_bytes=64)
+            src = weight_raw[g, h][:].rearrange("p j (a i t) -> p a t i j", i=2, t=PACK)
+            dst = grouped[:].rearrange("p t (a i j) -> p a t i j", i=2, j=PACK)
+            if vector_slots > 0:
+                nc.vector.tensor_copy(out=dst[:, :, :vector_slots], in_=src[:, :, :vector_slots])
+            if vector_slots < PACK:
+                nc.scalar.copy(out=dst[:, :, vector_slots:], in_=src[:, :, vector_slots:])
+            weight_grouped[g, h] = grouped
+
+        def quantize_weight(g, h):
+            codes = keep.tile([P, K_PASS], U32, name="weight_codes%d_%d" % (g, h), align_bytes=64)
+            scales = keep.tile([P, K_PASS], U8, name="weight_scales%d_%d" % (g, h), align_bytes=64)
+            quantize(codes[:], scales[:], weight_grouped[g, h][:].rearrange("p t c -> p (t c)"))
+            weight_codes[g, h], weight_scales[g, h] = codes, scales
+
+        def mx_pass(out, g, h, t, codes, scales, start, stop):
+            cols = slice(P * t, P * (t + 1))
+            nc.tensor.matmul_mx(
+                out=out,
+                lhsT=weight_codes[g, h][:, cols].bitcast(FP8X4),
+                lhsT_scale=weight_scales[g, h][:, cols],
+                rhs=codes.bitcast(FP8X4),
+                rhs_scale=scales,
+                start=start,
+                stop=stop,
+            )
+
+        text_codes = keep.tile([P, B], U32, name="text_codes", align_bytes=64)
+        text_scales = keep.tile([P, B], U8, name="text_scales", align_bytes=64)
+        cond_bank, offset_sb, offset_turn, offset_ps = {}, {}, {}, {}
+
+        def project_text(g):
+            bank = psum.tile([P, PACK * B], F32, name="turn", tag="turn", bufs=2)
+            for t in range(PACK):
+                mx_pass(bank[:, B * t : B * (t + 1)], g, PASSES, t, text_codes[:], text_scales[:], True, True)
+            cond_bank[g] = bank
+
+        def add_shift(g):
+            sb = keep.tile([P, PACK * B], F32, name="offset_sb%d" % g)
+            nc.vector.tensor_tensor(
+                out=sb[:], in0=cond_bank[g][:], in1=shift_sb[g][:].rearrange("p t b -> p (t b)"), op=ALU.add
+            )
+            offset_sb[g] = sb
+
+        def offset_out(g):
+            bank = psum.tile([P, PACK * P], F32, name="turn", tag="turn", bufs=2)
+            for t in range(PACK):
+                nc.tensor.transpose(bank[:, P * t : P * (t + 1)], offset_sb[g][:, B * t : B * (t + 1)], ident[:])
+            sb = keep.tile([P, PACK * P], F32, name="offset_turn%d" % g)
+            nc.scalar.copy(out=sb[:], in_=bank[:])
+            offset_turn[g] = sb
+
+        def offset_back(g):
+            bank = psum.tile([P, PACK * B], F32, name="offset_ps%d" % g)
+            for t in range(PACK):
+                nc.tensor.transpose(bank[:, B * t : B * (t + 1)], offset_turn[g][:, P * t : P * (t + 1)], ident[:])
+            offset_ps[g] = bank
+
+        banks, y_sb, y_bf, grouped = {}, {}, {}, {}
+
+        def columns(unit):
+            g, first, count = unit
+            return slice(PAIR * first, PAIR * (first + count))
+
+        def multiply_slot(unit, t, passes):
+            g, first, count = unit
+            c, at = divmod(PAIR * first, CHUNK)
+            cols = slice(at, at + PAIR * count)
+            for h in passes:
+                if h == 0:
+                    banks[unit, t] = psum.tile([P, PAIR * count], F32, name="acc%d" % t, tag="acc%d" % t)
+                mx_pass(
+                    banks[unit, t][:], g, h, t, patch_codes[:, c, h, cols], patch_scales[:, c, h, cols],
+                    h == 0, h == PASSES - 1,
+                )
+
+        def multiply(unit):
+            for t in range(PACK):
+                multiply_slot(unit, t, range(PASSES))
+
+        def per_image(values, unit, t, lo, hi):
+            first = B * t + PAIR * unit[1] // T
+            return values[:, first + lo : first + hi].unsqueeze(2).to_broadcast([P, hi - lo, T])
+
+        def y_part(unit, t, lo, hi):
+            return y_sb[unit][:, t, T * lo : T * hi].rearrange("p (b j) -> p b j", j=T)
+
+        def store_y(unit, t0, t1):
+            dst = y_out[K_PASS * unit[0] : K_PASS * (unit[0] + 1), columns(unit)]
+            nc.sync.dma_start(
+                out=dst.rearrange("(p t) m -> p t m", t=PACK)[:, t0:t1, :], in_=y_sb[unit][:, t0:t1, :]
+            )
+
+        def modulate(units, pool_images, scalar_slots, ahead, in_psum, fine, mid=None):
+            for n, unit in enumerate(units):
+                g = unit[0]
+                images = PAIR * unit[2] // T
+                y_sb[unit] = stage.tile([P, PACK, PAIR * unit[2]], F32, name="y", bufs=6)
+                scale_g = scale_sb[g][:].rearrange("p t b -> p (t b)")
+                following = units[n + 1] if n + 1 < len(units) else ahead
+                for t in range(PACK):
+                    if (n, t) in scalar_slots:
+                        for b in range(images):
+                            col = B * t + PAIR * unit[1] // T + b
+                            nc.scalar.activation(
+                                out=y_sb[unit][:, t, T * b : T * (b + 1)], in_=banks[unit, t][:, T * b : T * (b + 1)],
+                                func=ACT.Identity, scale=gain[g][:, col : col + 1], bias=offset_sb[g][:, col : col + 1],
+                            )
+                    else:
+                        nc.vector.scalar_tensor_tensor(
+                            out=y_part(unit, t, 0, images), in0=per_image(scale_g, unit, t, 0, images), scalar=1.0,
+                            in1=banks[unit, t][:].rearrange("p (b j) -> p b j", j=T),
+                            op0=ALU.add, op1=ALU.mult,
+                        )
+                        share = pool_images[n][t]
+                        if share > 0:
+                            part = y_part(unit, t, 0, share)
+                            nc.gpsimd.tensor_tensor(
+                                out=part, in0=part, in1=per_image(offset_sb[g][:], unit, t, 0, share), op=ALU.add
+                            )
+                    if following is not None:
+                        multiply_slot(following, t, range(PASSES))
+            if mid is not None:
+                mid()
+            for n, unit in enumerate(units):
+                images = PAIR * unit[2] // T
+                offset = offset_ps[unit[0]] if in_psum else offset_sb[unit[0]]
+                for t in range(PACK):
+                    share = pool_images[n][t]
+                    if (n, t) not in scalar_slots and share < images:
+                        part = y_part(unit, t, share, images)
+                        nc.vector.tensor_tensor(
+                            out=part, in0=part, in1=per_image(offset[:], unit, t, share, images), op=ALU.add
+                        )
+            for unit in units:
+                if fine and unit == units[-1]:
+                    store_y(unit, 0, 2)
+                    store_y(unit, 2, PACK)
+                else:
+                    store_y(unit, 0, PACK)
+
+        gain = {}
+
+        def make_gain(g):
+            sb = keep.tile([P, PACK * B], F32, name="gain%d" % g)
+            nc.scalar.activation(out=sb[:], in_=scale_sb[g][:].rearrange("p t b -> p (t b)"), func=ACT.Identity, bias=1.0)
+            gain[g] = sb
+
+        def round_y(unit, vector_cols):
+            rounded = stage.tile([P, PAIR * unit[2] * PACK], BF16, name="y_bf", bufs=4, align_bytes=64)
+            dst = rounded[:].rearrange("p (a i t) -> p a t i", i=2, t=PACK)
+            src = y_sb[unit][:].rearrange("p t (a i) -> p a t i", i=2)
+            half = vector_cols // 2
+            if half > 0:
+                nc.vector.tensor_copy(out=dst[:, :half], in_=src[:, :half])
+            nc.scalar.copy(out=dst[:, half:], in_=src[:, half:])
+            y_bf[unit] = rounded
+
+        y_scales = keep.tile([P, M], U8, name="y_scales", align_bytes=64)
+
+        def quantize_y(unit):
+            g, cols = unit[0], columns(unit)
+            codes = stage.tile([P, PAIR * unit[2]], U32, name="y_codes", bufs=4, align_bytes=64)
+            quantize(codes[:], y_scales[4 * g :, cols], y_bf[unit][:])
+            nc.sync.dma_start(out=words_out[g, :, cols], in_=codes[:].bitcast(I32))
+
+        def store_scales():
+            for q in range(4):
+                queue = nc.scalar if q % 2 else nc.sync
+                queue.dma_start(
+                    out=scales_out[:, 4 * q : 4 * q + 4, :],
+                    in_=y_scales[32 * q : 32 * q + 4 * GROUPS, :].bitcast(I32),
+                )
+
+        def turn_pair(pair):
+            if pair < 2:
+                grouped[pair] = stage.tile([P, PASSES, 2 * PAIR], F32, name="patch_grouped", bufs=4, align_bytes=64)
+                tile, at = grouped[pair], 0
+            else:
+                if pair % 2 == 0:
+                    grouped[pair] = stage.tile([P, PASSES, 2 * CHUNK], F32, name="patch_grouped", bufs=4, align_bytes=64)
+                tile, at = grouped[pair - pair % 2], 2 * (pair % 2)
+            for n in range(2):
+                turn_patch_tile(2 * pair + n, tile, at + n)
+
+        def quantize_patches(pair):
+            if pair < 2:
+                cols = slice(PAIR * pair, PAIR * (pair + 1))
+                for h in range(PASSES):
+                    quantize(patch_codes[:, 0, h, cols], patch_scales[:, 0, h, cols], grouped[pair][:, h, :].bitcast(BF16))
+            else:
+                quantize(
+                    patch_codes[:, pair // 2].rearrange("p h m -> p (h m)"),
+                    patch_scales[:, pair // 2].rearrange("p h m -> p (h m)"),
+                    grouped[pair][:].rearrange("p h w -> p (h w)").bitcast(BF16),
+                )
+
+        text_grouped = keep.tile([P, 1, 2 * B], F32, name="text_grouped", align_bytes=64)
+
+        def quantize_text():
+            quantize(text_codes[:], text_scales[:], text_grouped[:, 0, :].bitcast(BF16))
+
+        u = [(0, 0, 1), (0, 1, 1), (1, 0, 2), (0, 2, 2), (1, 2, 2), (0, 4, 2), (1, 4, 2), (0, 6, 2), (1, 6, 1), (1, 7, 1)]
+
+        interleave_weight(0, 0, 4)
+        turn_pair(0)
+        quantize_weight(0, 0)
+        interleave_weight(0, PASSES, 3)
+        turn(text_raw[:], 1, text_grouped[:])
+        quantize_patches(0)
+        quantize_weight(0, PASSES)
+        interleave_weight(0, 1, 3)
+        quantize_text()
+        project_text(0)
+        quantize_weight(0, 1)
+        add_shift(0)
+        multiply(u[0])
+        interleave_weight(1, PASSES, 0)
+        modulate([u[0]], [[16, 0, 0, 0]], [], None, False, False)
+        turn_pair(1)
+        offset_out(0)
+        turn_pair(2)
+        interleave_weight(1, 0, 3)
+        quantize_weight(1, PASSES)
+        project_text(1)
+        offset_back(0)
+        quantize_patches(1)
+        multiply(u[1])
+        interleave_weight(1, 1, 3)
+        quantize_weight(1, 0)
+        add_shift(1)
+        offset_out(1)
+        quantize_weight(1, 1)
+
+        round_y(u[0], 0)
+        modulate([u[1], u[2]], [[16, 16, 16, 16], [32, 0, 0, 0]], [], None, True, False, lambda: offset_back(1))
+        turn_pair(3)
+        turn_pair(4)
+        quantize_patches(2)
+        multiply(u[3])
+        quantize_y(u[0])
+        round_y(u[1], 0)
+        round_y(u[2], 0)
+        modulate([u[3], u[4]], [[32, 32, 32, 32], [16, 0, 0, 0]], [], None, True, False)
+        turn_pair(5)
+        turn_pair(6)
+        quantize_patches(4)
+        multiply(u[5])
+        quantize_y(u[2])
+        quantize_y(u[1])
+        round_y(u[3], 0)
+        round_y(u[4], 0)
+        modulate([u[5], u[6]], [[32, 32, 32, 32], [16, 0, 0, 0]], [], None, True, False)
+        turn_pair(7)
+        quantize_y(u[3])
+        quantize_patches(6)
+        multiply(u[7])
+        quantize_y(u[4])
+        round_y(u[5], 0)
+        round_y(u[6], 0)
+        modulate([u[7]], [[32, 32, 0, 0]], [], u[8], True, False)
+        round_y(u[7], 0)
+        quantize_y(u[5])
+        modulate([u[8]], [[16, 16, 0, 0]], [], u[9], True, False)
+        quantize_y(u[6])
+        round_y(u[8], 0)
+        modulate([u[9]], [[16, 16, 0, 0]], [], None, True, False)
+        round_y(u[9], 160)
+        quantize_y(u[7])
+        quantize_y(u[8])
+        quantize_y(u[9])
+        store_scales()

@@ -80,15 +80,20 @@ def tile_patch_modulate_text_planes_g2_kernel(
         load_weight(0, 1)
         load_modulation(0)
         load_weight(1, PASSES)
-        load_patches(1)
         load_weight(1, 0)
-        load_patches(2)
         load_weight(1, 1)
         load_modulation(1)
-        for pair in range(3, 8):
-            load_patches(pair)
+        load_patches(1)
+        load_patches(2)
+        load_patches(3)
+        load_patches(4)
+        load_patches(5)
+        load_patches(6)
+        load_patches(7)
 
-        def turn(raw_row, passes, dst_words):
+        turned = {}
+
+        def turn(key, raw_row, passes):
             bank = psum.tile([P, passes * 2 * P], F32, name="turn", tag="turn", bufs=2)
             words = raw_row.bitcast(F32)
             for h in range(passes):
@@ -97,32 +102,31 @@ def tile_patch_modulate_text_planes_g2_kernel(
                     nc.tensor.transpose(
                         bank[:, col : col + P], words[:, 2 * P * h + u : 2 * P * (h + 1) : 2], ident[:]
                     )
+            turned[key] = bank
+
+        def empty(key, passes, dst_words):
             nc.scalar.copy(
                 out=dst_words.rearrange("p h (m u) -> p h m u", u=2),
-                in_=bank[:].rearrange("p (h u m) -> p h m u", h=passes, u=2),
+                in_=turned[key][:].rearrange("p (h u m) -> p h m u", h=passes, u=2),
             )
 
         patch_codes = keep.tile([P, CHUNKS, PASSES, CHUNK], U32, name="patch_codes", align_bytes=64)
         patch_scales = keep.tile([P, CHUNKS, PASSES, CHUNK], U8, name="patch_scales", align_bytes=64)
-
-        def turn_patch_tile(tile_no, grouped, at):
-            raw = patch_raw[tile_no // 2]
-            turn(raw[:, tile_no % 2, :], PASSES, grouped[:, :, 2 * P * at : 2 * P * (at + 1)])
 
         def quantize(codes, scales, values):
             nc.vector.quantize_mx(out=codes.bitcast(FP8X4), scales=scales, in_=values)
 
         weight_grouped, weight_codes, weight_scales = {}, {}, {}
 
-        def interleave_weight(g, h, vector_slots):
-            grouped = stage.tile([P, PACK, K_PASS], BF16, name="weight_grouped", bufs=4, align_bytes=64)
-            src = weight_raw[g, h][:].rearrange("p j (a i t) -> p a t i j", i=2, t=PACK)
-            dst = grouped[:].rearrange("p t (a i j) -> p a t i j", i=2, j=PACK)
-            if vector_slots > 0:
-                nc.vector.tensor_copy(out=dst[:, :, :vector_slots], in_=src[:, :, :vector_slots])
-            if vector_slots < PACK:
-                nc.scalar.copy(out=dst[:, :, vector_slots:], in_=src[:, :, vector_slots:])
-            weight_grouped[g, h] = grouped
+        def interleave(g, h, engine, t0, t1):
+            if (g, h) not in weight_grouped:
+                weight_grouped[g, h] = stage.tile([P, PACK, K_PASS], BF16, name="weight_grouped", bufs=6, align_bytes=64)
+            src = weight_raw[g, h][:].rearrange("p j (a i t) -> p a t i j", i=2, t=PACK)[:, :, t0:t1]
+            dst = weight_grouped[g, h][:].rearrange("p t (a i j) -> p a t i j", i=2, j=PACK)[:, :, t0:t1]
+            if engine == "V":
+                nc.vector.tensor_copy(out=dst, in_=src)
+            else:
+                nc.scalar.copy(out=dst, in_=src)
 
         def quantize_weight(g, h):
             codes = keep.tile([P, K_PASS], U32, name="weight_codes%d_%d" % (g, h), align_bytes=64)
@@ -191,6 +195,10 @@ def tile_patch_modulate_text_planes_g2_kernel(
                     h == 0, h == PASSES - 1,
                 )
 
+        def multiply_pass(unit, h):
+            for t in range(PACK):
+                multiply_slot(unit, t, [h])
+
         def multiply(unit):
             for t in range(PACK):
                 multiply_slot(unit, t, range(PASSES))
@@ -256,6 +264,60 @@ def tile_patch_modulate_text_planes_g2_kernel(
                 else:
                     store_y(unit, 0, PACK)
 
+        def images_of(unit):
+            return PAIR * unit[2] // T
+
+        def scale_slot(unit, t, share, ahead):
+            g, images = unit[0], images_of(unit)
+            nc.vector.scalar_tensor_tensor(
+                out=y_part(unit, t, 0, images),
+                in0=per_image(scale_sb[g][:].rearrange("p t b -> p (t b)"), unit, t, 0, images), scalar=1.0,
+                in1=banks[unit, t][:].rearrange("p (b j) -> p b j", j=T),
+                op0=ALU.add, op1=ALU.mult,
+            )
+            if share > 0:
+                part = y_part(unit, t, 0, share)
+                nc.gpsimd.tensor_tensor(
+                    out=part, in0=part, in1=per_image(offset_sb[g][:], unit, t, 0, share), op=ALU.add
+                )
+            if ahead is not None:
+                multiply_slot(ahead, t, range(PASSES))
+
+        def offset_slot(unit, t, share, offsets):
+            images = images_of(unit)
+            if share < images:
+                part = y_part(unit, t, share, images)
+                nc.vector.tensor_tensor(
+                    out=part, in0=part, in1=per_image(offsets[unit[0]][:], unit, t, share, images), op=ALU.add
+                )
+
+        def step(unit, shares, before, ahead, offsets, mid=None, last=False, early=False, split=False):
+            y_sb[unit] = stage.tile([P, PACK, PAIR * unit[2]], F32, name="y", bufs=6)
+            for t in range(PACK - 1):
+                scale_slot(unit, t, shares[t], ahead)
+            if before is not None:
+                offset_slot(before, PACK - 1, 0, offsets)
+                store_y(before, PACK - 1 if early else 0, PACK)
+            if mid is not None:
+                mid()
+            if last:
+                scale_slot(unit, PACK - 1, 0, ahead)
+            for t in range(PACK - 1):
+                offset_slot(unit, t, shares[t], offsets)
+            if last:
+                offset_slot(unit, PACK - 1, 0, offsets)
+                store_y(unit, 0, 2)
+                store_y(unit, 2, PACK)
+            else:
+                scale_slot(unit, PACK - 1, 0, ahead)
+                if split:
+                    store_y(unit, 0, PACK - 1)
+
+        def warm(n, t):
+            bank = psum.tile([P, CHUNK], F32, name="acc%d" % t, tag="acc%d" % t)
+            for k in range(n):
+                mx_pass(bank[:], 0, 0, 0, weight_codes[0, 0][:], weight_scales[0, 0][:], True, True)
+
         gain = {}
 
         def make_gain(g):
@@ -270,7 +332,8 @@ def tile_patch_modulate_text_planes_g2_kernel(
             half = vector_cols // 2
             if half > 0:
                 nc.vector.tensor_copy(out=dst[:, :half], in_=src[:, :half])
-            nc.scalar.copy(out=dst[:, half:], in_=src[:, half:])
+            if vector_cols < PAIR * unit[2]:
+                nc.scalar.copy(out=dst[:, half:], in_=src[:, half:])
             y_bf[unit] = rounded
 
         y_scales = keep.tile([P, M], U8, name="y_scales", align_bytes=64)
@@ -290,100 +353,113 @@ def tile_patch_modulate_text_planes_g2_kernel(
                 )
 
         def turn_pair(pair):
-            if pair < 2:
-                grouped[pair] = stage.tile([P, PASSES, 2 * PAIR], F32, name="patch_grouped", bufs=4, align_bytes=64)
-                tile, at = grouped[pair], 0
-            else:
-                if pair % 2 == 0:
-                    grouped[pair] = stage.tile([P, PASSES, 2 * CHUNK], F32, name="patch_grouped", bufs=4, align_bytes=64)
-                tile, at = grouped[pair - pair % 2], 2 * (pair % 2)
             for n in range(2):
-                turn_patch_tile(2 * pair + n, tile, at + n)
+                turn((pair, n), patch_raw[pair][:, n, :], PASSES)
 
-        def quantize_patches(pair):
-            if pair < 2:
-                cols = slice(PAIR * pair, PAIR * (pair + 1))
-                for h in range(PASSES):
-                    quantize(patch_codes[:, 0, h, cols], patch_scales[:, 0, h, cols], grouped[pair][:, h, :].bitcast(BF16))
-            else:
-                quantize(
-                    patch_codes[:, pair // 2].rearrange("p h m -> p (h m)"),
-                    patch_scales[:, pair // 2].rearrange("p h m -> p (h m)"),
-                    grouped[pair][:].rearrange("p h w -> p (h w)").bitcast(BF16),
-                )
+        def empty_pair(pair):
+            grouped[pair] = stage.tile([P, PASSES, 2 * PAIR], F32, name="patch_grouped", bufs=4, align_bytes=64)
+            for n in range(2):
+                empty((pair, n), PASSES, grouped[pair][:, :, 2 * P * n : 2 * P * (n + 1)])
+
+        def pair_in(pair):
+            turn_pair(pair)
+            empty_pair(pair)
+
+        def text_in():
+            turn("text", text_raw[:], 1)
+            empty("text", 1, text_grouped[:])
+
+        def quantize_pair(pair):
+            c, at = divmod(PAIR * pair, CHUNK)
+            for h in range(PASSES):
+                cols = slice(at, at + PAIR)
+                quantize(patch_codes[:, c, h, cols], patch_scales[:, c, h, cols], grouped[pair][:, h, :].bitcast(BF16))
 
         text_grouped = keep.tile([P, 1, 2 * B], F32, name="text_grouped", align_bytes=64)
 
         def quantize_text():
             quantize(text_codes[:], text_scales[:], text_grouped[:, 0, :].bitcast(BF16))
 
-        u = [(0, 0, 1), (0, 1, 1), (1, 0, 2), (0, 2, 2), (1, 2, 2), (0, 4, 2), (1, 4, 2), (0, 6, 2), (1, 6, 1), (1, 7, 1)]
+        u = [(0, 0, 1), (1, 0, 1), (0, 1, 1), (1, 1, 1), (0, 2, 2), (1, 2, 2), (0, 4, 2), (1, 4, 2), (0, 6, 2), (1, 6, 1), (1, 7, 1)]
+        X = PASSES
+        half, full = [16, 16, 0], [32, 32, 0]
 
-        interleave_weight(0, 0, 4)
-        turn_pair(0)
+        interleave(0, 0, "V", 0, 3)
+        interleave(0, 0, "S", 3, 4)
         quantize_weight(0, 0)
-        interleave_weight(0, PASSES, 3)
-        turn(text_raw[:], 1, text_grouped[:])
-        quantize_patches(0)
-        quantize_weight(0, PASSES)
-        interleave_weight(0, 1, 3)
+        interleave(0, X, "V", 0, 3)
+        interleave(0, X, "S", 3, 4)
+        pair_in(0)
+        quantize_weight(0, X)
+        interleave(0, 1, "V", 0, 3)
+        interleave(0, 1, "S", 3, 4)
+        text_in()
+        warm(3, 0)
+        quantize_pair(0)
         quantize_text()
         project_text(0)
         quantize_weight(0, 1)
         add_shift(0)
         multiply(u[0])
-        interleave_weight(1, PASSES, 0)
-        modulate([u[0]], [[16, 0, 0, 0]], [], None, False, False)
-        turn_pair(1)
+        interleave(1, X, "S", 0, 4)
+        step(u[0], [16, 0, 0], None, None, offset_sb)
         offset_out(0)
-        turn_pair(2)
-        interleave_weight(1, 0, 3)
-        quantize_weight(1, PASSES)
-        project_text(1)
+
+        interleave(1, 0, "V", 0, 2)
+        interleave(1, 0, "S", 2, 4)
         offset_back(0)
-        quantize_patches(1)
-        multiply(u[1])
-        interleave_weight(1, 1, 3)
+        pair_in(1)
+        offset_slot(u[0], 3, 0, offset_sb)
+        store_y(u[0], 0, PACK)
+        quantize_weight(1, X)
+        interleave(1, 1, "S", 3, 4)
+        project_text(1)
+
         quantize_weight(1, 0)
+        multiply_pass(u[1], 0)
+        interleave(1, 1, "V", 0, 3)
         add_shift(1)
         offset_out(1)
         quantize_weight(1, 1)
-
+        multiply_pass(u[1], 1)
+        quantize_pair(1)
+        offset_back(1)
+        pair_in(2)
         round_y(u[0], 0)
-        modulate([u[1], u[2]], [[16, 16, 16, 16], [32, 0, 0, 0]], [], None, True, False, lambda: offset_back(1))
-        turn_pair(3)
-        turn_pair(4)
-        quantize_patches(2)
-        multiply(u[3])
+        step(u[1], half, None, u[2], offset_ps, lambda: pair_in(3), False, True, True)
+        quantize_pair(2)
         quantize_y(u[0])
+        step(u[2], half, u[1], u[3], offset_ps, lambda: pair_in(4), False, True, True)
         round_y(u[1], 0)
+        quantize_pair(3)
+        step(u[3], half, u[2], u[4], offset_ps, lambda: pair_in(5), False, True, True)
         round_y(u[2], 0)
-        modulate([u[3], u[4]], [[32, 32, 32, 32], [16, 0, 0, 0]], [], None, True, False)
-        turn_pair(5)
-        turn_pair(6)
-        quantize_patches(4)
-        multiply(u[5])
-        quantize_y(u[2])
+        quantize_pair(4)
         quantize_y(u[1])
+        step(u[4], full, u[3], u[5], offset_ps, lambda: pair_in(6), False, True, True)
         round_y(u[3], 0)
+        quantize_pair(5)
+        quantize_y(u[2])
+        step(u[5], full, u[4], u[6], offset_ps, lambda: pair_in(7), False, True, True)
         round_y(u[4], 0)
-        modulate([u[5], u[6]], [[32, 32, 32, 32], [16, 0, 0, 0]], [], None, True, False)
-        turn_pair(7)
+        quantize_pair(6)
         quantize_y(u[3])
-        quantize_patches(6)
-        multiply(u[7])
-        quantize_y(u[4])
+        step(u[6], full, u[5], u[7], offset_ps, None, False, True, True)
         round_y(u[5], 0)
+        quantize_pair(7)
+        quantize_y(u[4])
+
+        step(u[7], full, u[6], u[8], offset_ps, None, False, True, True)
         round_y(u[6], 0)
-        modulate([u[7]], [[32, 32, 0, 0]], [], u[8], True, False)
-        round_y(u[7], 0)
         quantize_y(u[5])
-        modulate([u[8]], [[16, 16, 0, 0]], [], u[9], True, False)
+        step(u[8], full, u[7], u[9], offset_ps, None, False, True, True)
+        round_y(u[7], 0)
         quantize_y(u[6])
-        round_y(u[8], 0)
-        modulate([u[9]], [[16, 16, 0, 0]], [], None, True, False)
-        round_y(u[9], 160)
+        step(u[9], half, u[8], u[10], offset_ps, lambda: round_y(u[8], 0), False, True, True)
         quantize_y(u[7])
+        step(u[10], half, u[9], None, offset_ps, lambda: round_y(u[9], 0), True, True, True)
         quantize_y(u[8])
+        round_y(u[10], 256)
         quantize_y(u[9])
+        quantize_y(u[10])
         store_scales()

@@ -53,9 +53,9 @@ def tile_patch_modulate_text_planes_g2_kernel(
         patch_raw, weight_raw, scale_sb, shift_sb = {}, {}, {}, {}
 
         def load_patches(pair):
-            raw = keep.tile([P, 2, K], BF16, name="patch_raw%d" % pair)
+            raw = keep.tile([P, 2 * K], BF16, name="patch_raw%d" % pair)
             src = rows[2 * P * pair : 2 * P * (pair + 1), :]
-            nc.sync.dma_start(out=raw[:], in_=src.rearrange("(n p) k -> p n k", p=P))
+            nc.sync.dma_start(out=raw[:], in_=src.rearrange("(p n) k -> p (n k)", n=2))
             patch_raw[pair] = raw
 
         def load_weight(g, h):
@@ -63,27 +63,38 @@ def tile_patch_modulate_text_planes_g2_kernel(
             raw = keep.tile([P, PACK, K_PASS], BF16, name="weight_raw%d_%d" % (g, h))
             src = w[:, K_PASS * g : K_PASS * (g + 1)]
             nc.sync.dma_start(out=raw[:], in_=src.rearrange("(p j) c -> p j c", j=PACK))
-            weight_raw[g, h] = raw
+            weight_raw[g, h] = raw[:]
+
+        def load_weight_rows(h):
+            w = w_text if h == PASSES else w_patch[K_PASS * h : K_PASS * (h + 1), :]
+            raw = keep.tile([P, PACK, D], BF16, name="weight_rows%d" % h)
+            nc.sync.dma_start(out=raw[:], in_=w.rearrange("(p j) c -> p j c", j=PACK))
+            for g in range(GROUPS):
+                weight_raw[g, h] = raw[:, :, K_PASS * g : K_PASS * (g + 1)]
+
+        def load_per_image(name, src, dst):
+            sb = keep.tile([P, GROUPS, PACK * B], BF16, name=name)
+            nc.sync.dma_start(out=sb[:], in_=src.rearrange("(g p t) b -> p g (t b)", p=P, t=PACK))
+            for g in range(GROUPS):
+                dst[g] = sb[:, g, :]
 
         def load_modulation(g):
             for name, src, dst in (("scale", scale, scale_sb), ("shift", shift, shift_sb)):
                 sb = keep.tile([P, PACK, B], BF16, name="%s%d" % (name, g))
                 part = src[K_PASS * g : K_PASS * (g + 1), :]
                 nc.sync.dma_start(out=sb[:], in_=part.rearrange("(p t) b -> p t b", t=PACK))
-                dst[g] = sb
+                dst[g] = sb[:].rearrange("p t b -> p (t b)")
 
         text_raw = keep.tile([P, KT], BF16, name="text_raw")
         load_weight(0, 0)
         load_patches(0)
-        load_weight(0, PASSES)
-        nc.sync.dma_start(out=text_raw[:], in_=text)
-        load_weight(0, 1)
-        load_modulation(0)
-        load_weight(1, PASSES)
         load_weight(1, 0)
-        load_weight(1, 1)
-        load_modulation(1)
+        nc.sync.dma_start(out=text_raw[:], in_=text)
+        load_weight_rows(PASSES)
         load_patches(1)
+        load_weight_rows(1)
+        load_per_image("shift", shift, shift_sb)
+        load_per_image("scale", scale, scale_sb)
         load_patches(2)
         load_patches(3)
         load_patches(4)
@@ -93,21 +104,18 @@ def tile_patch_modulate_text_planes_g2_kernel(
 
         turned = {}
 
-        def turn(key, raw_row, passes):
-            bank = psum.tile([P, passes * 2 * P], F32, name="turn", tag="turn", bufs=2)
-            words = raw_row.bitcast(F32)
-            for h in range(passes):
+        def turn(key, word_runs):
+            bank = psum.tile([P, len(word_runs) * 2 * P], F32, name="turn", tag="turn", bufs=2)
+            for n, words in enumerate(word_runs):
                 for u in range(2):
-                    col = (2 * h + u) * P
-                    nc.tensor.transpose(
-                        bank[:, col : col + P], words[:, 2 * P * h + u : 2 * P * (h + 1) : 2], ident[:]
-                    )
+                    col = (2 * n + u) * P
+                    nc.tensor.transpose(bank[:, col : col + P], words[:, u : 2 * P : 2], ident[:])
             turned[key] = bank
 
-        def empty(key, passes, dst_words):
+        def empty(key, dst_words):
             nc.scalar.copy(
-                out=dst_words.rearrange("p h (m u) -> p h m u", u=2),
-                in_=turned[key][:].rearrange("p (h u m) -> p h m u", h=passes, u=2),
+                out=dst_words.rearrange("p (m w) -> p m w", m=P),
+                in_=turned[key][:].rearrange("p (w m) -> p m w", m=P),
             )
 
         patch_codes = keep.tile([P, CHUNKS, PASSES, CHUNK], U32, name="patch_codes", align_bytes=64)
@@ -121,7 +129,7 @@ def tile_patch_modulate_text_planes_g2_kernel(
         def interleave(g, h, engine, t0, t1):
             if (g, h) not in weight_grouped:
                 weight_grouped[g, h] = stage.tile([P, PACK, K_PASS], BF16, name="weight_grouped", bufs=6, align_bytes=64)
-            src = weight_raw[g, h][:].rearrange("p j (a i t) -> p a t i j", i=2, t=PACK)[:, :, t0:t1]
+            src = weight_raw[g, h].rearrange("p j (a i t) -> p a t i j", i=2, t=PACK)[:, :, t0:t1]
             dst = weight_grouped[g, h][:].rearrange("p t (a i j) -> p a t i j", i=2, j=PACK)[:, :, t0:t1]
             if engine == "V":
                 nc.vector.tensor_copy(out=dst, in_=src)
@@ -151,7 +159,7 @@ def tile_patch_modulate_text_planes_g2_kernel(
         cond_bank, offset_sb, offset_turn, offset_ps = {}, {}, {}, {}
 
         def project_text(g):
-            bank = psum.tile([P, PACK * B], F32, name="turn", tag="turn", bufs=2)
+            bank = psum.tile([P, PACK * B], F32, name="acc%d" % (2 + g), tag="acc%d" % (2 + g))
             for t in range(PACK):
                 mx_pass(bank[:, B * t : B * (t + 1)], g, PASSES, t, text_codes[:], text_scales[:], True, True)
             cond_bank[g] = bank
@@ -159,7 +167,7 @@ def tile_patch_modulate_text_planes_g2_kernel(
         def add_shift(g):
             sb = keep.tile([P, PACK * B], F32, name="offset_sb%d" % g)
             nc.vector.tensor_tensor(
-                out=sb[:], in0=cond_bank[g][:], in1=shift_sb[g][:].rearrange("p t b -> p (t b)"), op=ALU.add
+                out=sb[:], in0=cond_bank[g][:], in1=shift_sb[g], op=ALU.add
             )
             offset_sb[g] = sb
 
@@ -221,7 +229,7 @@ def tile_patch_modulate_text_planes_g2_kernel(
                 g = unit[0]
                 images = PAIR * unit[2] // T
                 y_sb[unit] = stage.tile([P, PACK, PAIR * unit[2]], F32, name="y", bufs=6)
-                scale_g = scale_sb[g][:].rearrange("p t b -> p (t b)")
+                scale_g = scale_sb[g]
                 following = units[n + 1] if n + 1 < len(units) else ahead
                 for t in range(PACK):
                     if (n, t) in scalar_slots:
@@ -267,12 +275,26 @@ def tile_patch_modulate_text_planes_g2_kernel(
         def images_of(unit):
             return PAIR * unit[2] // T
 
+        fused = {}
+
+        def fuse_slot(unit, count):
+            g, t = unit[0], PACK - 1
+            fused[unit] = count
+            for b in range(count):
+                col = B * t + PAIR * unit[1] // T + b
+                nc.scalar.activation(
+                    out=y_sb[unit][:, t, T * b : T * (b + 1)], in_=banks[unit, t][:, T * b : T * (b + 1)],
+                    func=ACT.Identity, scale=gain[g][:, col : col + 1], bias=offset_sb[g][:, col : col + 1],
+                )
+
         def scale_slot(unit, t, share, ahead):
             g, images = unit[0], images_of(unit)
-            nc.vector.scalar_tensor_tensor(
-                out=y_part(unit, t, 0, images),
-                in0=per_image(scale_sb[g][:].rearrange("p t b -> p (t b)"), unit, t, 0, images), scalar=1.0,
-                in1=banks[unit, t][:].rearrange("p (b j) -> p b j", j=T),
+            lo = fused.get(unit, 0) if t == PACK - 1 else 0
+            if lo < images:
+              nc.vector.scalar_tensor_tensor(
+                out=y_part(unit, t, lo, images),
+                in0=per_image(scale_sb[g], unit, t, lo, images), scalar=1.0,
+                in1=banks[unit, t][:, T * lo :].rearrange("p (b j) -> p b j", j=T),
                 op0=ALU.add, op1=ALU.mult,
             )
             if share > 0:
@@ -285,14 +307,17 @@ def tile_patch_modulate_text_planes_g2_kernel(
 
         def offset_slot(unit, t, share, offsets):
             images = images_of(unit)
+            if t == PACK - 1:
+                share = fused.get(unit, 0)
             if share < images:
                 part = y_part(unit, t, share, images)
                 nc.vector.tensor_tensor(
                     out=part, in0=part, in1=per_image(offsets[unit[0]][:], unit, t, share, images), op=ALU.add
                 )
 
-        def step(unit, shares, before, ahead, offsets, mid=None, last=False, early=False, split=False):
+        def step(unit, shares, before, ahead, offsets, mid=None, last=False, early=False, split=False, fma=0):
             y_sb[unit] = stage.tile([P, PACK, PAIR * unit[2]], F32, name="y", bufs=6)
+            fuse_slot(unit, fma)
             for t in range(PACK - 1):
                 scale_slot(unit, t, shares[t], ahead)
             if before is not None:
@@ -322,14 +347,14 @@ def tile_patch_modulate_text_planes_g2_kernel(
 
         def make_gain(g):
             sb = keep.tile([P, PACK * B], F32, name="gain%d" % g)
-            nc.scalar.activation(out=sb[:], in_=scale_sb[g][:].rearrange("p t b -> p (t b)"), func=ACT.Identity, bias=1.0)
+            nc.scalar.activation(out=sb[:], in_=scale_sb[g], func=ACT.Identity, bias=1.0)
             gain[g] = sb
 
         def round_y(unit, vector_cols):
             rounded = stage.tile([P, PAIR * unit[2] * PACK], BF16, name="y_bf", bufs=4, align_bytes=64)
-            dst = rounded[:].rearrange("p (a i t) -> p a t i", i=2, t=PACK)
-            src = y_sb[unit][:].rearrange("p t (a i) -> p a t i", i=2)
-            half = vector_cols // 2
+            dst = rounded[:].rearrange("p (m t) -> p m t", t=PACK)
+            src = y_sb[unit][:].rearrange("p t m -> p m t")
+            half = vector_cols
             if half > 0:
                 nc.vector.tensor_copy(out=dst[:, :half], in_=src[:, :half])
             if vector_cols < PAIR * unit[2]:
@@ -352,114 +377,106 @@ def tile_patch_modulate_text_planes_g2_kernel(
                     in_=y_scales[32 * q : 32 * q + 4 * GROUPS, :].bitcast(I32),
                 )
 
-        def turn_pair(pair):
-            for n in range(2):
-                turn((pair, n), patch_raw[pair][:, n, :], PASSES)
-
-        def empty_pair(pair):
-            grouped[pair] = stage.tile([P, PASSES, 2 * PAIR], F32, name="patch_grouped", bufs=4, align_bytes=64)
-            for n in range(2):
-                empty((pair, n), PASSES, grouped[pair][:, :, 2 * P * n : 2 * P * (n + 1)])
-
         def pair_in(pair):
-            turn_pair(pair)
-            empty_pair(pair)
+            words = patch_raw[pair][:].bitcast(F32).rearrange("p (n h w) -> p n h w", n=2, h=PASSES)
+            for h in range(PASSES):
+                turn((pair, h), [words[:, n, h, :] for n in range(2)])
+                grouped[pair, h] = stage.tile([P, 2 * PAIR], F32, name="patch_grouped", bufs=8, align_bytes=64)
+                empty((pair, h), grouped[pair, h][:])
 
         def text_in():
-            turn("text", text_raw[:], 1)
-            empty("text", 1, text_grouped[:])
+            turn("text", [text_raw[:].bitcast(F32)])
+            empty("text", text_grouped[:, 0, :])
 
         def quantize_pair(pair):
             c, at = divmod(PAIR * pair, CHUNK)
             for h in range(PASSES):
                 cols = slice(at, at + PAIR)
-                quantize(patch_codes[:, c, h, cols], patch_scales[:, c, h, cols], grouped[pair][:, h, :].bitcast(BF16))
+                quantize(patch_codes[:, c, h, cols], patch_scales[:, c, h, cols], grouped[pair, h][:].bitcast(BF16))
 
         text_grouped = keep.tile([P, 1, 2 * B], F32, name="text_grouped", align_bytes=64)
 
         def quantize_text():
             quantize(text_codes[:], text_scales[:], text_grouped[:, 0, :].bitcast(BF16))
 
-        u = [(0, 0, 1), (1, 0, 1), (0, 1, 1), (1, 1, 1), (0, 2, 2), (1, 2, 2), (0, 4, 2), (1, 4, 2), (0, 6, 2), (1, 6, 1), (1, 7, 1)]
+        u = [(0, 0, 2), (1, 0, 2), (0, 2, 2), (1, 2, 2), (0, 4, 2), (1, 4, 2), (0, 6, 2), (1, 6, 1), (1, 7, 1)]
         X = PASSES
-        half, full = [16, 16, 0], [32, 32, 0]
+        half, full = [16, 8, 0], [32, 26, 0]
 
         interleave(0, 0, "V", 0, 3)
         interleave(0, 0, "S", 3, 4)
         quantize_weight(0, 0)
-        interleave(0, X, "V", 0, 3)
-        interleave(0, X, "S", 3, 4)
+        interleave(1, 0, "V", 0, 3)
+        interleave(1, 0, "S", 3, 4)
         pair_in(0)
-        quantize_weight(0, X)
-        interleave(0, 1, "V", 0, 3)
-        interleave(0, 1, "S", 3, 4)
         text_in()
-        warm(3, 0)
-        quantize_pair(0)
-        quantize_text()
-        project_text(0)
-        quantize_weight(0, 1)
-        add_shift(0)
-        multiply(u[0])
-        interleave(1, X, "S", 0, 4)
-        step(u[0], [16, 0, 0], None, None, offset_sb)
-        offset_out(0)
-
-        interleave(1, 0, "V", 0, 2)
-        interleave(1, 0, "S", 2, 4)
-        offset_back(0)
-        pair_in(1)
-        offset_slot(u[0], 3, 0, offset_sb)
-        store_y(u[0], 0, PACK)
-        quantize_weight(1, X)
-        interleave(1, 1, "S", 3, 4)
-        project_text(1)
 
         quantize_weight(1, 0)
-        multiply_pass(u[1], 0)
-        interleave(1, 1, "V", 0, 3)
-        add_shift(1)
-        offset_out(1)
-        quantize_weight(1, 1)
-        multiply_pass(u[1], 1)
-        quantize_pair(1)
-        offset_back(1)
-        pair_in(2)
-        round_y(u[0], 0)
-        step(u[1], half, None, u[2], offset_ps, lambda: pair_in(3), False, True, True)
-        quantize_pair(2)
-        quantize_y(u[0])
-        step(u[2], half, u[1], u[3], offset_ps, lambda: pair_in(4), False, True, True)
-        round_y(u[1], 0)
-        quantize_pair(3)
-        step(u[3], half, u[2], u[4], offset_ps, lambda: pair_in(5), False, True, True)
-        round_y(u[2], 0)
-        quantize_pair(4)
-        quantize_y(u[1])
-        step(u[4], full, u[3], u[5], offset_ps, lambda: pair_in(6), False, True, True)
-        round_y(u[3], 0)
-        quantize_pair(5)
-        quantize_y(u[2])
-        step(u[5], full, u[4], u[6], offset_ps, lambda: pair_in(7), False, True, True)
-        round_y(u[4], 0)
-        quantize_pair(6)
-        quantize_y(u[3])
-        step(u[6], full, u[5], u[7], offset_ps, None, False, True, True)
-        round_y(u[5], 0)
-        quantize_pair(7)
-        quantize_y(u[4])
+        quantize_pair(0)
+        quantize_text()
+        interleave(0, X, "V", 0, 3)
+        interleave(0, X, "S", 3, 4)
+        interleave(1, X, "V", 0, 2)
+        interleave(1, X, "S", 2, 4)
+        pair_in(1)
 
-        step(u[7], full, u[6], u[8], offset_ps, None, False, True, True)
-        round_y(u[6], 0)
+        quantize_weight(0, X)
+        project_text(0)
+        quantize_weight(1, X)
+        project_text(1)
+        quantize_pair(1)
+        interleave(0, 1, "S", 3, 4)
+        interleave(1, 1, "S", 1, 4)
+        interleave(0, 1, "V", 0, 3)
+        add_shift(0)
+        multiply_slot(u[0], 0, [0])
+        multiply_slot(u[0], 1, [0])
+        multiply_slot(u[0], 2, [0])
+        offset_out(0)
+        quantize_weight(0, 1)
+        interleave(1, 1, "V", 0, 1)
+        add_shift(1)
+        multiply_slot(u[0], 0, [1])
+        multiply_slot(u[0], 1, [1])
+        multiply_slot(u[0], 2, [1])
+        multiply_slot(u[0], 3, [0, 1])
+        offset_back(0)
+        quantize_weight(1, 1)
+        pair_in(2)
+        y_sb[u[0]] = stage.tile([P, PACK, CHUNK], F32, name="y", bufs=6)
+        scale_slot(u[0], 0, full[0], u[1])
+        pair_in(3)
+        scale_slot(u[0], 1, full[1], u[1])
+        scale_slot(u[0], 2, full[2], u[1])
+        offset_slot(u[0], 1, full[1], offset_ps)
+        offset_slot(u[0], 2, full[2], offset_ps)
+        offset_out(1)
+        scale_slot(u[0], 3, 0, u[1])
+        store_y(u[0], 0, 3)
+        quantize_pair(2)
+        quantize_pair(3)
+        offset_back(1)
+        pair_in(4)
+        step(u[1], full, u[0], u[2], offset_ps, lambda: (round_y(u[0], 0), pair_in(5)), False, True, True)
+        quantize_pair(4)
+        step(u[2], full, u[1], u[3], offset_ps, lambda: (round_y(u[1], 0), pair_in(6)), False, True, True)
+        quantize_pair(5)
+        quantize_y(u[0])
+        step(u[3], full, u[2], u[4], offset_ps, lambda: (round_y(u[2], 0), pair_in(7)), False, True, True)
+        quantize_pair(6)
+        quantize_y(u[1])
+        step(u[4], full, u[3], u[5], offset_ps, lambda: round_y(u[3], 0), False, True, True)
+        quantize_pair(7)
+        quantize_y(u[2])
+        step(u[5], full, u[4], u[6], offset_ps, lambda: round_y(u[4], 0), False, True, True)
+        quantize_y(u[3])
+        step(u[6], full, u[5], u[7], offset_ps, lambda: round_y(u[5], 0), False, True, True)
+        quantize_y(u[4])
+        step(u[7], half, u[6], u[8], offset_ps, lambda: round_y(u[6], 0), False, True, True)
         quantize_y(u[5])
-        step(u[8], full, u[7], u[9], offset_ps, None, False, True, True)
-        round_y(u[7], 0)
+        step(u[8], half, u[7], None, offset_ps, lambda: round_y(u[7], 0), True, True, True)
         quantize_y(u[6])
-        step(u[9], half, u[8], u[10], offset_ps, lambda: round_y(u[8], 0), False, True, True)
+        round_y(u[8], 256)
         quantize_y(u[7])
-        step(u[10], half, u[9], None, offset_ps, lambda: round_y(u[9], 0), True, True, True)
         quantize_y(u[8])
-        round_y(u[10], 256)
-        quantize_y(u[9])
-        quantize_y(u[10])
         store_scales()

@@ -14,29 +14,31 @@ U32 = mybir.dt.uint32
 U8 = mybir.dt.uint8
 FP8X4 = mybir.dt.float8_e4m3fn_x4
 ALU = mybir.AluOpType
-ACT = mybir.ActivationFunctionType
+IDENTITY = mybir.ActivationFunctionType.Identity
 
 P = 128
 PACK = 4
 K_PASS = P * PACK
 PASSES = K // K_PASS
+TEXT = PASSES
 GROUPS = D // K_PASS
-CHUNK = 512
-CHUNKS = M // CHUNK
-IMAGES = CHUNK // T
-ROW_TILES = CHUNK // P
-PAIR = 2 * P
-UNITS = GROUPS * CHUNKS
-POOL_SLOTS = 2
-HEAD_VECTOR_SLOTS = 3
-TAIL_VECTOR_COLS = 320
+SHEET = 2 * P
+SHEETS = M // SHEET
+BANK = 512
+LAST_SLOT = PACK - 1
+SCALE_ROWS = 4
+
+VECTOR_SLOTS = {(0, 0): 3, (1, 0): 3, (0, TEXT): 3, (1, TEXT): 2, (0, 1): 3, (1, 1): 1}
+LEFT_IN_SLOT_2 = {2: 6, 1: 8}
+FUSED = (0, 4, 10)
+NOT_FUSED = (0, 0, 0)
 
 
 def tile_patch_modulate_text_planes_g2_kernel(
     tc, patches, w_patch, text, w_text, scale, shift, out_0, out_1, out_2
 ):
     nc = tc.nc
-    rows = patches.rearrange("b j k -> (b j) k")
+    patch_rows = patches.rearrange("b j k -> (b j) k")
     y_out = out_0.rearrange("d b j -> d (b j)")
     words_out = out_1.rearrange("g p m t -> g p (m t)").bitcast(I32)
     scales_out = out_2.bitcast(I32)
@@ -50,96 +52,102 @@ def tile_patch_modulate_text_planes_g2_kernel(
         ident = keep.tile([P, P], F32, name="ident")
         make_identity(nc, ident[:])
 
-        patch_raw, weight_raw, scale_sb, shift_sb = {}, {}, {}, {}
+        patch_raw, weight_raw = {}, {}
 
-        def load_patches(pair):
-            raw = keep.tile([P, 2 * K], BF16, name="patch_raw%d" % pair)
-            src = rows[2 * P * pair : 2 * P * (pair + 1), :]
+        def load_sheet(sheet):
+            raw = keep.tile([P, 2 * K], BF16, name="patch_raw%d" % sheet)
+            src = patch_rows[SHEET * sheet : SHEET * (sheet + 1), :]
             nc.sync.dma_start(out=raw[:], in_=src.rearrange("(p n) k -> p (n k)", n=2))
-            patch_raw[pair] = raw
+            patch_raw[sheet] = raw
 
-        def load_weight(g, h):
-            w = w_text if h == PASSES else w_patch[K_PASS * h : K_PASS * (h + 1), :]
-            raw = keep.tile([P, PACK, K_PASS], BF16, name="weight_raw%d_%d" % (g, h))
-            src = w[:, K_PASS * g : K_PASS * (g + 1)]
-            nc.sync.dma_start(out=raw[:], in_=src.rearrange("(p j) c -> p j c", j=PACK))
-            weight_raw[g, h] = raw[:]
+        def load_weight(h, groups):
+            w = w_text if h == TEXT else w_patch[K_PASS * h : K_PASS * (h + 1), :]
+            first, width = K_PASS * groups[0], K_PASS * len(groups)
+            raw = keep.tile([P, PACK, width], BF16, name="weight_raw%d_%d" % (groups[0], h))
+            nc.sync.dma_start(out=raw[:], in_=w[:, first : first + width].rearrange("(p j) c -> p j c", j=PACK))
+            for n, g in enumerate(groups):
+                weight_raw[g, h] = raw[:, :, K_PASS * n : K_PASS * (n + 1)]
 
-        def load_weight_rows(h):
-            w = w_text if h == PASSES else w_patch[K_PASS * h : K_PASS * (h + 1), :]
-            raw = keep.tile([P, PACK, D], BF16, name="weight_rows%d" % h)
-            nc.sync.dma_start(out=raw[:], in_=w.rearrange("(p j) c -> p j c", j=PACK))
-            for g in range(GROUPS):
-                weight_raw[g, h] = raw[:, :, K_PASS * g : K_PASS * (g + 1)]
-
-        def load_per_image(name, src, dst):
+        def load_per_image(name, src):
             sb = keep.tile([P, GROUPS, PACK * B], BF16, name=name)
             nc.sync.dma_start(out=sb[:], in_=src.rearrange("(g p t) b -> p g (t b)", p=P, t=PACK))
-            for g in range(GROUPS):
-                dst[g] = sb[:, g, :]
+            return sb
 
-        def load_modulation(g):
-            for name, src, dst in (("scale", scale, scale_sb), ("shift", shift, shift_sb)):
-                sb = keep.tile([P, PACK, B], BF16, name="%s%d" % (name, g))
-                part = src[K_PASS * g : K_PASS * (g + 1), :]
-                nc.sync.dma_start(out=sb[:], in_=part.rearrange("(p t) b -> p t b", t=PACK))
-                dst[g] = sb[:].rearrange("p t b -> p (t b)")
-
+        load_weight(0, [0])
+        load_sheet(0)
+        load_weight(0, [1])
         text_raw = keep.tile([P, KT], BF16, name="text_raw")
-        load_weight(0, 0)
-        load_patches(0)
-        load_weight(1, 0)
         nc.sync.dma_start(out=text_raw[:], in_=text)
-        load_weight_rows(PASSES)
-        load_patches(1)
-        load_weight_rows(1)
-        load_per_image("shift", shift, shift_sb)
-        load_per_image("scale", scale, scale_sb)
-        load_patches(2)
-        load_patches(3)
-        load_patches(4)
-        load_patches(5)
-        load_patches(6)
-        load_patches(7)
-
-        turned = {}
-
-        def turn(key, word_runs):
-            bank = psum.tile([P, len(word_runs) * 2 * P], F32, name="turn", tag="turn", bufs=2)
-            for n, words in enumerate(word_runs):
-                for u in range(2):
-                    col = (2 * n + u) * P
-                    nc.tensor.transpose(bank[:, col : col + P], words[:, u : 2 * P : 2], ident[:])
-            turned[key] = bank
-
-        def empty(key, dst_words):
-            nc.scalar.copy(
-                out=dst_words.rearrange("p (m w) -> p m w", m=P),
-                in_=turned[key][:].rearrange("p (w m) -> p m w", m=P),
-            )
-
-        patch_codes = keep.tile([P, CHUNKS, PASSES, CHUNK], U32, name="patch_codes", align_bytes=64)
-        patch_scales = keep.tile([P, CHUNKS, PASSES, CHUNK], U8, name="patch_scales", align_bytes=64)
+        load_weight(TEXT, [0, 1])
+        load_sheet(1)
+        load_weight(1, [0, 1])
+        shift_sb = load_per_image("shift_sb", shift)
+        scale_sb = load_per_image("scale_sb", scale)
+        for sheet in range(2, SHEETS):
+            load_sheet(sheet)
 
         def quantize(codes, scales, values):
             nc.vector.quantize_mx(out=codes.bitcast(FP8X4), scales=scales, in_=values)
 
-        weight_grouped, weight_codes, weight_scales = {}, {}, {}
+        def turn(word_rows, sorted_words):
+            bank = psum.tile([P, len(word_rows) * 2 * P], F32, name="turn", bufs=2)
+            for n, words in enumerate(word_rows):
+                for u in range(2):
+                    col = (2 * n + u) * P
+                    nc.tensor.transpose(bank[:, col : col + P], words[:, u : 2 * P : 2], ident[:])
+            nc.scalar.copy(
+                out=sorted_words.rearrange("p (r w) -> p r w", r=P),
+                in_=bank[:].rearrange("p (w r) -> p r w", r=P),
+            )
 
-        def interleave(g, h, engine, t0, t1):
-            if (g, h) not in weight_grouped:
-                weight_grouped[g, h] = stage.tile([P, PACK, K_PASS], BF16, name="weight_grouped", bufs=6, align_bytes=64)
-            src = weight_raw[g, h].rearrange("p j (a i t) -> p a t i j", i=2, t=PACK)[:, :, t0:t1]
-            dst = weight_grouped[g, h][:].rearrange("p t (a i j) -> p a t i j", i=2, j=PACK)[:, :, t0:t1]
-            if engine == "V":
-                nc.vector.tensor_copy(out=dst, in_=src)
-            else:
-                nc.scalar.copy(out=dst, in_=src)
+        patch_codes = keep.tile([P, M // BANK, PASSES, BANK], U32, name="patch_codes", align_bytes=64)
+        patch_scales = keep.tile([P, M // BANK, PASSES, BANK], U8, name="patch_scales", align_bytes=64)
+        patch_sorted = {}
+
+        def turn_sheet(sheet):
+            words = patch_raw[sheet][:].bitcast(F32).rearrange("p (n h w) -> p n h w", n=2, h=PASSES)
+            for h in range(PASSES):
+                dst = stage.tile([P, 2 * SHEET], F32, name="patch_sorted", bufs=4 * PASSES, align_bytes=64)
+                turn([words[:, n, h, :] for n in range(2)], dst[:])
+                patch_sorted[sheet, h] = dst
+
+        def patch_operand(first_sheet, sheets, h):
+            c, at = divmod(SHEET * first_sheet, BANK)
+            cols = slice(at, at + SHEET * sheets)
+            return patch_codes[:, c, h, cols], patch_scales[:, c, h, cols]
+
+        def quantize_sheet(sheet):
+            for h in range(PASSES):
+                codes, scales = patch_operand(sheet, 1, h)
+                quantize(codes, scales, patch_sorted[sheet, h][:].bitcast(BF16))
+
+        text_sorted = keep.tile([P, 2 * B], F32, name="text_sorted", align_bytes=64)
+        text_codes = keep.tile([P, B], U32, name="text_codes", align_bytes=64)
+        text_scales = keep.tile([P, B], U8, name="text_scales", align_bytes=64)
+
+        weight_sorted, weight_codes, weight_scales = {}, {}, {}
+
+        def sort_views(g, h, slots):
+            if (g, h) not in weight_sorted:
+                weight_sorted[g, h] = keep.tile(
+                    [P, PACK, K_PASS], BF16, name="weight_sorted%d_%d" % (g, h), align_bytes=64
+                )
+            dst = weight_sorted[g, h][:].rearrange("p t (a i j) -> p a t i j", i=2, j=PACK)
+            src = weight_raw[g, h].rearrange("p j (a i t) -> p a t i j", i=2, t=PACK)
+            return dst[:, :, slots], src[:, :, slots]
+
+        def sort_on_vector(g, h):
+            dst, src = sort_views(g, h, slice(0, VECTOR_SLOTS[g, h]))
+            nc.vector.tensor_copy(out=dst, in_=src)
+
+        def sort_on_scalar(g, h):
+            dst, src = sort_views(g, h, slice(VECTOR_SLOTS[g, h], PACK))
+            nc.scalar.copy(out=dst, in_=src)
 
         def quantize_weight(g, h):
             codes = keep.tile([P, K_PASS], U32, name="weight_codes%d_%d" % (g, h), align_bytes=64)
             scales = keep.tile([P, K_PASS], U8, name="weight_scales%d_%d" % (g, h), align_bytes=64)
-            quantize(codes[:], scales[:], weight_grouped[g, h][:].rearrange("p t c -> p (t c)"))
+            quantize(codes[:], scales[:], weight_sorted[g, h][:].rearrange("p t c -> p (t c)"))
             weight_codes[g, h], weight_scales[g, h] = codes, scales
 
         def mx_pass(out, g, h, t, codes, scales, start, stop):
@@ -154,69 +162,106 @@ def tile_patch_modulate_text_planes_g2_kernel(
                 stop=stop,
             )
 
-        text_codes = keep.tile([P, B], U32, name="text_codes", align_bytes=64)
-        text_scales = keep.tile([P, B], U8, name="text_scales", align_bytes=64)
-        cond_bank, offset_sb, offset_turn, offset_ps = {}, {}, {}, {}
+        def slot_bank(t, width):
+            return psum.tile([P, width], F32, name="slot%d" % t)
+
+        text_bank, offset_sb, offset_turned, offset_ps = {}, {}, {}, {}
 
         def project_text(g):
-            bank = psum.tile([P, PACK * B], F32, name="acc%d" % (2 + g), tag="acc%d" % (2 + g))
+            bank = slot_bank(PACK - GROUPS + g, PACK * B)
             for t in range(PACK):
-                mx_pass(bank[:, B * t : B * (t + 1)], g, PASSES, t, text_codes[:], text_scales[:], True, True)
-            cond_bank[g] = bank
+                mx_pass(bank[:, B * t : B * (t + 1)], g, TEXT, t, text_codes[:], text_scales[:], True, True)
+            text_bank[g] = bank
 
         def add_shift(g):
             sb = keep.tile([P, PACK * B], F32, name="offset_sb%d" % g)
-            nc.vector.tensor_tensor(
-                out=sb[:], in0=cond_bank[g][:], in1=shift_sb[g], op=ALU.add
-            )
+            nc.vector.tensor_tensor(out=sb[:], in0=text_bank[g][:], in1=shift_sb[:, g, :], op=ALU.add)
             offset_sb[g] = sb
 
-        def offset_out(g):
-            bank = psum.tile([P, PACK * P], F32, name="turn", tag="turn", bufs=2)
+        def transpose_slots(bank, src):
             for t in range(PACK):
-                nc.tensor.transpose(bank[:, P * t : P * (t + 1)], offset_sb[g][:, B * t : B * (t + 1)], ident[:])
-            sb = keep.tile([P, PACK * P], F32, name="offset_turn%d" % g)
+                nc.tensor.transpose(bank[:, P * t : P * (t + 1)], src[:, P * t : P * (t + 1)], ident[:])
+
+        def offset_out(g):
+            bank = psum.tile([P, PACK * P], F32, name="turn", bufs=2)
+            transpose_slots(bank, offset_sb[g])
+            sb = keep.tile([P, PACK * P], F32, name="offset_turned%d" % g)
             nc.scalar.copy(out=sb[:], in_=bank[:])
-            offset_turn[g] = sb
+            offset_turned[g] = sb
 
         def offset_back(g):
             bank = psum.tile([P, PACK * B], F32, name="offset_ps%d" % g)
-            for t in range(PACK):
-                nc.tensor.transpose(bank[:, B * t : B * (t + 1)], offset_turn[g][:, P * t : P * (t + 1)], ident[:])
+            transpose_slots(bank, offset_turned[g])
             offset_ps[g] = bank
 
-        banks, y_sb, y_bf, grouped = {}, {}, {}, {}
+        banks, y_sb, y_bf, fused_of = {}, {}, {}, {}
 
         def columns(unit):
-            g, first, count = unit
-            return slice(PAIR * first, PAIR * (first + count))
+            return slice(SHEET * unit[1], SHEET * (unit[1] + unit[2]))
 
-        def multiply_slot(unit, t, passes):
-            g, first, count = unit
-            c, at = divmod(PAIR * first, CHUNK)
-            cols = slice(at, at + PAIR * count)
+        def images_of(unit):
+            return SHEET * unit[2] // T
+
+        def multiply(unit, t, passes):
+            g, first_sheet, sheets = unit
             for h in passes:
                 if h == 0:
-                    banks[unit, t] = psum.tile([P, PAIR * count], F32, name="acc%d" % t, tag="acc%d" % t)
-                mx_pass(
-                    banks[unit, t][:], g, h, t, patch_codes[:, c, h, cols], patch_scales[:, c, h, cols],
-                    h == 0, h == PASSES - 1,
-                )
+                    banks[unit, t] = slot_bank(t, SHEET * sheets)
+                codes, scales = patch_operand(first_sheet, sheets, h)
+                mx_pass(banks[unit, t][:], g, h, t, codes, scales, h == 0, h == PASSES - 1)
 
-        def multiply_pass(unit, h):
-            for t in range(PACK):
-                multiply_slot(unit, t, [h])
-
-        def multiply(unit):
-            for t in range(PACK):
-                multiply_slot(unit, t, range(PASSES))
+        def image_column(unit, t, b):
+            return B * t + SHEET * unit[1] // T + b
 
         def per_image(values, unit, t, lo, hi):
-            first = B * t + PAIR * unit[1] // T
-            return values[:, first + lo : first + hi].unsqueeze(2).to_broadcast([P, hi - lo, T])
+            cols = values[:, image_column(unit, t, lo) : image_column(unit, t, hi)]
+            return cols.unsqueeze(2).to_broadcast([P, hi - lo, T])
 
-        def y_part(unit, t, lo, hi):
-            return y_sb[unit][:, t, T * lo : T * hi].rearrange("p (b j) -> p b j", j=T)
+        def by_image(tile_row, lo, hi):
+            return tile_row[:, T * lo : T * hi].rearrange("p (b j) -> p b j", j=T)
+
+        def pool_images(unit, t):
+            left = fused_of[unit][2] or LEFT_IN_SLOT_2[unit[2]]
+            return {0: images_of(unit), 2: images_of(unit) - left}.get(t, 0)
+
+        def vector_images(unit, t):
+            return images_of(unit) - (fused_of[unit][t] if t < LAST_SLOT else 0)
+
+        def scale_slot(unit, t, following):
+            g, y_t, bank = unit[0], y_sb[unit][:, t, :], banks[unit, t][:]
+            hi, share = vector_images(unit, t), pool_images(unit, t)
+            nc.vector.scalar_tensor_tensor(
+                out=by_image(y_t, 0, hi),
+                in0=per_image(scale_sb[:, g, :], unit, t, 0, hi),
+                scalar=1.0,
+                in1=by_image(bank, 0, hi),
+                op0=ALU.add,
+                op1=ALU.mult,
+            )
+            for b in range(hi, images_of(unit)):
+                col = image_column(unit, t, b)
+                nc.scalar.activation(
+                    out=y_t[:, T * b : T * (b + 1)],
+                    in_=bank[:, T * b : T * (b + 1)],
+                    func=IDENTITY,
+                    scale=gain[:, g, col : col + 1],
+                    bias=offset_sb[g][:, col : col + 1],
+                )
+            if share > 0:
+                part = by_image(y_t, 0, share)
+                nc.gpsimd.tensor_tensor(
+                    out=part, in0=part, in1=per_image(offset_sb[g][:], unit, t, 0, share), op=ALU.add
+                )
+            if following is not None:
+                multiply(following, t, range(PASSES))
+
+        def offset_slot(unit, t):
+            lo, hi = pool_images(unit, t), vector_images(unit, t)
+            if lo < hi:
+                part = by_image(y_sb[unit][:, t, :], lo, hi)
+                nc.vector.tensor_tensor(
+                    out=part, in0=part, in1=per_image(offset_ps[unit[0]][:], unit, t, lo, hi), op=ALU.add
+                )
 
         def store_y(unit, t0, t1):
             dst = y_out[K_PASS * unit[0] : K_PASS * (unit[0] + 1), columns(unit)]
@@ -224,259 +269,113 @@ def tile_patch_modulate_text_planes_g2_kernel(
                 out=dst.rearrange("(p t) m -> p t m", t=PACK)[:, t0:t1, :], in_=y_sb[unit][:, t0:t1, :]
             )
 
-        def modulate(units, pool_images, scalar_slots, ahead, in_psum, fine, mid=None):
-            for n, unit in enumerate(units):
-                g = unit[0]
-                images = PAIR * unit[2] // T
-                y_sb[unit] = stage.tile([P, PACK, PAIR * unit[2]], F32, name="y", bufs=6)
-                scale_g = scale_sb[g]
-                following = units[n + 1] if n + 1 < len(units) else ahead
-                for t in range(PACK):
-                    if (n, t) in scalar_slots:
-                        for b in range(images):
-                            col = B * t + PAIR * unit[1] // T + b
-                            nc.scalar.activation(
-                                out=y_sb[unit][:, t, T * b : T * (b + 1)], in_=banks[unit, t][:, T * b : T * (b + 1)],
-                                func=ACT.Identity, scale=gain[g][:, col : col + 1], bias=offset_sb[g][:, col : col + 1],
-                            )
-                    else:
-                        nc.vector.scalar_tensor_tensor(
-                            out=y_part(unit, t, 0, images), in0=per_image(scale_g, unit, t, 0, images), scalar=1.0,
-                            in1=banks[unit, t][:].rearrange("p (b j) -> p b j", j=T),
-                            op0=ALU.add, op1=ALU.mult,
-                        )
-                        share = pool_images[n][t]
-                        if share > 0:
-                            part = y_part(unit, t, 0, share)
-                            nc.gpsimd.tensor_tensor(
-                                out=part, in0=part, in1=per_image(offset_sb[g][:], unit, t, 0, share), op=ALU.add
-                            )
-                    if following is not None:
-                        multiply_slot(following, t, range(PASSES))
-            if mid is not None:
-                mid()
-            for n, unit in enumerate(units):
-                images = PAIR * unit[2] // T
-                offset = offset_ps[unit[0]] if in_psum else offset_sb[unit[0]]
-                for t in range(PACK):
-                    share = pool_images[n][t]
-                    if (n, t) not in scalar_slots and share < images:
-                        part = y_part(unit, t, share, images)
-                        nc.vector.tensor_tensor(
-                            out=part, in0=part, in1=per_image(offset[:], unit, t, share, images), op=ALU.add
-                        )
-            for unit in units:
-                if fine and unit == units[-1]:
-                    store_y(unit, 0, 2)
-                    store_y(unit, 2, PACK)
-                else:
-                    store_y(unit, 0, PACK)
-
-        def images_of(unit):
-            return PAIR * unit[2] // T
-
-        fused = {}
-
-        def fuse_slot(unit, count):
-            g, t = unit[0], PACK - 1
-            fused[unit] = count
-            for b in range(count):
-                col = B * t + PAIR * unit[1] // T + b
-                nc.scalar.activation(
-                    out=y_sb[unit][:, t, T * b : T * (b + 1)], in_=banks[unit, t][:, T * b : T * (b + 1)],
-                    func=ACT.Identity, scale=gain[g][:, col : col + 1], bias=offset_sb[g][:, col : col + 1],
-                )
-
-        def scale_slot(unit, t, share, ahead):
-            g, images = unit[0], images_of(unit)
-            lo = fused.get(unit, 0) if t == PACK - 1 else 0
-            if lo < images:
-              nc.vector.scalar_tensor_tensor(
-                out=y_part(unit, t, lo, images),
-                in0=per_image(scale_sb[g], unit, t, lo, images), scalar=1.0,
-                in1=banks[unit, t][:, T * lo :].rearrange("p (b j) -> p b j", j=T),
-                op0=ALU.add, op1=ALU.mult,
-            )
-            if share > 0:
-                part = y_part(unit, t, 0, share)
-                nc.gpsimd.tensor_tensor(
-                    out=part, in0=part, in1=per_image(offset_sb[g][:], unit, t, 0, share), op=ALU.add
-                )
-            if ahead is not None:
-                multiply_slot(ahead, t, range(PASSES))
-
-        def offset_slot(unit, t, share, offsets):
-            images = images_of(unit)
-            if t == PACK - 1:
-                share = fused.get(unit, 0)
-            if share < images:
-                part = y_part(unit, t, share, images)
-                nc.vector.tensor_tensor(
-                    out=part, in0=part, in1=per_image(offsets[unit[0]][:], unit, t, share, images), op=ALU.add
-                )
-
-        def step(unit, shares, before, ahead, offsets, mid=None, last=False, early=False, split=False, fma=0):
-            y_sb[unit] = stage.tile([P, PACK, PAIR * unit[2]], F32, name="y", bufs=6)
-            fuse_slot(unit, fma)
-            for t in range(PACK - 1):
-                scale_slot(unit, t, shares[t], ahead)
-            if before is not None:
-                offset_slot(before, PACK - 1, 0, offsets)
-                store_y(before, PACK - 1 if early else 0, PACK)
-            if mid is not None:
-                mid()
-            if last:
-                scale_slot(unit, PACK - 1, 0, ahead)
-            for t in range(PACK - 1):
-                offset_slot(unit, t, shares[t], offsets)
-            if last:
-                offset_slot(unit, PACK - 1, 0, offsets)
-                store_y(unit, 0, 2)
-                store_y(unit, 2, PACK)
-            else:
-                scale_slot(unit, PACK - 1, 0, ahead)
-                if split:
-                    store_y(unit, 0, PACK - 1)
-
-        def warm(n, t):
-            bank = psum.tile([P, CHUNK], F32, name="acc%d" % t, tag="acc%d" % t)
-            for k in range(n):
-                mx_pass(bank[:], 0, 0, 0, weight_codes[0, 0][:], weight_scales[0, 0][:], True, True)
-
-        gain = {}
-
-        def make_gain(g):
-            sb = keep.tile([P, PACK * B], F32, name="gain%d" % g)
-            nc.scalar.activation(out=sb[:], in_=scale_sb[g], func=ACT.Identity, bias=1.0)
-            gain[g] = sb
-
-        def round_y(unit, vector_cols):
-            rounded = stage.tile([P, PAIR * unit[2] * PACK], BF16, name="y_bf", bufs=4, align_bytes=64)
-            dst = rounded[:].rearrange("p (m t) -> p m t", t=PACK)
-            src = y_sb[unit][:].rearrange("p t m -> p m t")
-            half = vector_cols
-            if half > 0:
-                nc.vector.tensor_copy(out=dst[:, :half], in_=src[:, :half])
-            if vector_cols < PAIR * unit[2]:
-                nc.scalar.copy(out=dst[:, half:], in_=src[:, half:])
+        def rounding_views(unit):
+            rounded = stage.tile([P, SHEET * unit[2] * PACK], BF16, name="y_bf", bufs=4, align_bytes=64)
             y_bf[unit] = rounded
+            dst = rounded[:].rearrange("p (a i t) -> p a t i", i=2, t=PACK)
+            return dst, y_sb[unit][:].rearrange("p t (a i) -> p a t i", i=2)
 
         y_scales = keep.tile([P, M], U8, name="y_scales", align_bytes=64)
 
         def quantize_y(unit):
             g, cols = unit[0], columns(unit)
-            codes = stage.tile([P, PAIR * unit[2]], U32, name="y_codes", bufs=4, align_bytes=64)
-            quantize(codes[:], y_scales[4 * g :, cols], y_bf[unit][:])
+            codes = stage.tile([P, SHEET * unit[2]], U32, name="y_codes", bufs=4, align_bytes=64)
+            quantize(codes[:], y_scales[SCALE_ROWS * g :, cols], y_bf[unit][:])
             nc.sync.dma_start(out=words_out[g, :, cols], in_=codes[:].bitcast(I32))
 
-        def store_scales():
-            for q in range(4):
-                queue = nc.scalar if q % 2 else nc.sync
-                queue.dma_start(
-                    out=scales_out[:, 4 * q : 4 * q + 4, :],
-                    in_=y_scales[32 * q : 32 * q + 4 * GROUPS, :].bitcast(I32),
+        def store_scales(lo, hi, queues):
+            for quadrant in range(P // 32):
+                rows = slice(SCALE_ROWS * quadrant, SCALE_ROWS * (quadrant + 1))
+                live = y_scales[32 * quadrant : 32 * quadrant + SCALE_ROWS * GROUPS, lo:hi]
+                queues[quadrant % len(queues)].dma_start(
+                    out=scales_out[:, rows, lo // 4 : hi // 4], in_=live.bitcast(I32)
                 )
 
-        def pair_in(pair):
-            words = patch_raw[pair][:].bitcast(F32).rearrange("p (n h w) -> p n h w", n=2, h=PASSES)
-            for h in range(PASSES):
-                turn((pair, h), [words[:, n, h, :] for n in range(2)])
-                grouped[pair, h] = stage.tile([P, 2 * PAIR], F32, name="patch_grouped", bufs=8, align_bytes=64)
-                empty((pair, h), grouped[pair, h][:])
+        units = [(g, first, 2) for first in range(0, SHEETS, 2) for g in range(GROUPS)]
+        units = units[:-1] + [(GROUPS - 1, SHEETS - 2, 1), (GROUPS - 1, SHEETS - 1, 1)]
 
-        def text_in():
-            turn("text", [text_raw[:].bitcast(F32)])
-            empty("text", text_grouped[:, 0, :])
-
-        def quantize_pair(pair):
-            c, at = divmod(PAIR * pair, CHUNK)
-            for h in range(PASSES):
-                cols = slice(at, at + PAIR)
-                quantize(patch_codes[:, c, h, cols], patch_scales[:, c, h, cols], grouped[pair, h][:].bitcast(BF16))
-
-        text_grouped = keep.tile([P, 1, 2 * B], F32, name="text_grouped", align_bytes=64)
-
-        def quantize_text():
-            quantize(text_codes[:], text_scales[:], text_grouped[:, 0, :].bitcast(BF16))
-
-        u = [(0, 0, 2), (1, 0, 2), (0, 2, 2), (1, 2, 2), (0, 4, 2), (1, 4, 2), (0, 6, 2), (1, 6, 1), (1, 7, 1)]
-        X = PASSES
-        half, full = [16, 8, 0], [32, 26, 0]
-
-        interleave(0, 0, "V", 0, 3)
-        interleave(0, 0, "S", 3, 4)
+        sort_on_vector(0, 0)
+        first_dst, first_src = sort_views(0, 0, slice(VECTOR_SLOTS[0, 0], PACK))
+        nc.scalar.activation(out=first_dst, in_=first_src, func=IDENTITY)
         quantize_weight(0, 0)
-        interleave(1, 0, "V", 0, 3)
-        interleave(1, 0, "S", 3, 4)
-        pair_in(0)
-        text_in()
-
+        sort_on_vector(1, 0)
+        sort_on_scalar(1, 0)
+        turn_sheet(0)
+        turn([text_raw[:].bitcast(F32)], text_sorted[:])
         quantize_weight(1, 0)
-        quantize_pair(0)
-        quantize_text()
-        interleave(0, X, "V", 0, 3)
-        interleave(0, X, "S", 3, 4)
-        interleave(1, X, "V", 0, 2)
-        interleave(1, X, "S", 2, 4)
-        pair_in(1)
-
-        quantize_weight(0, X)
-        project_text(0)
-        quantize_weight(1, X)
-        project_text(1)
-        quantize_pair(1)
-        interleave(0, 1, "S", 3, 4)
-        interleave(1, 1, "S", 1, 4)
-        interleave(0, 1, "V", 0, 3)
+        quantize_sheet(0)
+        quantize(text_codes[:], text_scales[:], text_sorted[:].bitcast(BF16))
+        for g in range(GROUPS):
+            sort_on_vector(g, TEXT)
+            sort_on_scalar(g, TEXT)
+        turn_sheet(1)
+        for g in range(GROUPS):
+            quantize_weight(g, TEXT)
+            project_text(g)
+        quantize_sheet(1)
+        for g in range(GROUPS):
+            sort_on_scalar(g, 1)
+        sort_on_vector(0, 1)
         add_shift(0)
-        multiply_slot(u[0], 0, [0])
-        multiply_slot(u[0], 1, [0])
-        multiply_slot(u[0], 2, [0])
+        for t in range(LAST_SLOT):
+            multiply(units[0], t, [0])
         offset_out(0)
         quantize_weight(0, 1)
-        interleave(1, 1, "V", 0, 1)
+        sort_on_vector(1, 1)
         add_shift(1)
-        multiply_slot(u[0], 0, [1])
-        multiply_slot(u[0], 1, [1])
-        multiply_slot(u[0], 2, [1])
-        multiply_slot(u[0], 3, [0, 1])
+        for t in range(LAST_SLOT):
+            multiply(units[0], t, [1])
+        multiply(units[0], LAST_SLOT, range(PASSES))
         offset_back(0)
+        gain = keep.tile([P, GROUPS, PACK * B], F32, name="gain")
+        nc.scalar.activation(out=gain[:], in_=scale_sb[:], func=IDENTITY, bias=1.0)
         quantize_weight(1, 1)
-        pair_in(2)
-        y_sb[u[0]] = stage.tile([P, PACK, CHUNK], F32, name="y", bufs=6)
-        scale_slot(u[0], 0, full[0], u[1])
-        pair_in(3)
-        scale_slot(u[0], 1, full[1], u[1])
-        scale_slot(u[0], 2, full[2], u[1])
-        offset_slot(u[0], 1, full[1], offset_ps)
-        offset_slot(u[0], 2, full[2], offset_ps)
-        offset_out(1)
-        scale_slot(u[0], 3, 0, u[1])
-        store_y(u[0], 0, 3)
-        quantize_pair(2)
-        quantize_pair(3)
-        offset_back(1)
-        pair_in(4)
-        step(u[1], full, u[0], u[2], offset_ps, lambda: (round_y(u[0], 0), pair_in(5)), False, True, True)
-        quantize_pair(4)
-        step(u[2], full, u[1], u[3], offset_ps, lambda: (round_y(u[1], 0), pair_in(6)), False, True, True)
-        quantize_pair(5)
-        quantize_y(u[0])
-        step(u[3], full, u[2], u[4], offset_ps, lambda: (round_y(u[2], 0), pair_in(7)), False, True, True)
-        quantize_pair(6)
-        quantize_y(u[1])
-        step(u[4], full, u[3], u[5], offset_ps, lambda: round_y(u[3], 0), False, True, True)
-        quantize_pair(7)
-        quantize_y(u[2])
-        step(u[5], full, u[4], u[6], offset_ps, lambda: round_y(u[4], 0), False, True, True)
-        quantize_y(u[3])
-        step(u[6], full, u[5], u[7], offset_ps, lambda: round_y(u[5], 0), False, True, True)
-        quantize_y(u[4])
-        step(u[7], half, u[6], u[8], offset_ps, lambda: round_y(u[6], 0), False, True, True)
-        quantize_y(u[5])
-        step(u[8], half, u[7], None, offset_ps, lambda: round_y(u[7], 0), True, True, True)
-        quantize_y(u[6])
-        round_y(u[8], 256)
-        quantize_y(u[7])
-        quantize_y(u[8])
-        store_scales()
+        turn_sheet(2)
+
+        last_step = len(units) - 1
+        for s, unit in enumerate(units):
+            following = units[s + 1] if s < last_step else None
+            turning = s + 4 < SHEETS
+            fused_of[unit] = FUSED if unit[2] == 2 and not turning else NOT_FUSED
+            y_sb[unit] = stage.tile([P, PACK, SHEET * unit[2]], F32, name="y", bufs=6)
+            for t in range(LAST_SLOT):
+                scale_slot(unit, t, following)
+                if s == 0 and t == 0:
+                    turn_sheet(3)
+            if s == 0:
+                offset_out(1)
+            else:
+                offset_slot(units[s - 1], LAST_SLOT)
+                store_y(units[s - 1], LAST_SLOT, PACK)
+                dst, src = rounding_views(units[s - 1])
+                nc.scalar.copy(out=dst, in_=src)
+                if turning:
+                    turn_sheet(s + 4)
+            if s < last_step:
+                for t in range(LAST_SLOT):
+                    offset_slot(unit, t)
+                scale_slot(unit, LAST_SLOT, following)
+                store_y(unit, 0, LAST_SLOT)
+            else:
+                scale_slot(unit, LAST_SLOT, None)
+                for t in range(PACK):
+                    offset_slot(unit, t)
+                store_y(unit, 0, PACK // 2)
+                store_y(unit, PACK // 2, PACK)
+            if s == 0:
+                quantize_sheet(2)
+            if s + 3 < SHEETS:
+                quantize_sheet(s + 3)
+            if s == 0:
+                offset_back(1)
+                turn_sheet(4)
+            if s >= 2:
+                quantize_y(units[s - 2])
+            if s == last_step - 1:
+                store_scales(0, M - BANK, [nc.sync])
+
+        dst, src = rounding_views(units[last_step])
+        nc.vector.tensor_copy(out=dst, in_=src)
+        quantize_y(units[last_step - 1])
+        quantize_y(units[last_step])
+        store_scales(M - BANK, M, [nc.sync, nc.scalar])

@@ -283,13 +283,6 @@ def tile_patch_modulate_text_planes_g2_kernel(
             quantize(codes[:], y_scales[SCALE_ROWS * g :, cols], y_bf[unit][:])
             nc.sync.dma_start(out=words_out[g, :, cols], in_=codes[:].bitcast(I32))
 
-        def store_scales(lo, hi, queues):
-            for quadrant in range(P // 32):
-                rows = slice(SCALE_ROWS * quadrant, SCALE_ROWS * (quadrant + 1))
-                live = y_scales[32 * quadrant : 32 * quadrant + SCALE_ROWS * GROUPS, lo:hi]
-                queues[quadrant % len(queues)].dma_start(
-                    out=scales_out[:, rows, lo // 4 : hi // 4], in_=live.bitcast(I32)
-                )
 
         units = [(g, first, 2) for first in range(0, SHEETS, 2) for g in range(GROUPS)]
         units = units[:-1] + [(GROUPS - 1, SHEETS - 2, 1), (GROUPS - 1, SHEETS - 1, 1)]
@@ -371,11 +364,13 @@ def tile_patch_modulate_text_planes_g2_kernel(
                 turn_sheet(4)
             if s >= 2:
                 quantize_y(units[s - 2])
-            if s == last_step - 1:
-                store_scales(0, M - BANK, [nc.sync])
 
         dst, src = rounding_views(units[last_step])
         nc.vector.tensor_copy(out=dst, in_=src)
         quantize_y(units[last_step - 1])
         quantize_y(units[last_step])
-        store_scales(M - BANK, M, [nc.sync, nc.scalar])
+        for quadrant in range(P // 32):
+            rows = slice(SCALE_ROWS * quadrant, SCALE_ROWS * (quadrant + 1))
+            live = y_scales[32 * quadrant : 32 * quadrant + SCALE_ROWS * GROUPS, :]
+            queue = nc.scalar if quadrant % 2 else nc.sync
+            queue.dma_start(out=scales_out[:, rows, :], in_=live.bitcast(I32))

from contextlib import ExitStack

import concourse.mybir as mybir
from concourse.masks import make_identity

B, T, K, KT, D = 128, 16, 1024, 512, 1024
M = B * T
FLOPS = 2 * D * M * K + 2 * D * B * KT

F32 = mybir.dt.float32
BF16 = mybir.dt.bfloat16
I32 = mybir.dt.int32
U32 = mybir.dt.uint32
U8 = mybir.dt.uint8
FP8X4 = mybir.dt.float8_e4m3fn_x4
ALU = mybir.AluOpType
IDENTITY = mybir.ActivationFunctionType.Identity

P = 128
PACK = 4
K_PASS = P * PACK
PASSES = K // K_PASS
TEXT = PASSES
GROUPS = D // K_PASS
SHEET = 2 * P
SHEETS = M // SHEET
BANK = 512
LAST_SLOT = PACK - 1
SCALE_ROWS = 4

VECTOR_SLOTS = {(0, 0): 3, (1, 0): 3, (0, TEXT): 3, (1, TEXT): 2, (0, 1): 3, (1, 1): 1}
LEFT_IN_SLOT_2 = {2: 6, 1: 8}
FUSED = (0, 4, 10)
NOT_FUSED = (0, 0, 0)


def tile_patch_modulate_text_planes_g2_kernel(
    tc, patches, w_patch, text, w_text, scale, shift, out_0, out_1, out_2
):
    nc = tc.nc
    patch_rows = patches.rearrange("b j k -> (b j) k")
    y_out = out_0.rearrange("d b j -> d (b j)")
    words_out = out_1.rearrange("g p m t -> g p (m t)").bitcast(I32)
    scales_out = out_2.bitcast(I32)

    with ExitStack() as ctx:
        keep = ctx.enter_context(tc.tile_pool(name="keep", bufs=1))
        stage = ctx.enter_context(tc.tile_pool(name="stage", bufs=2))
        psum = ctx.enter_context(tc.psum_pool(name="psum", bufs=1))
        ctx.enter_context(tc.manual_schedule())

        ident = keep.tile([P, P], F32, name="ident")
        make_identity(nc, ident[:])

        patch_raw, weight_raw = {}, {}

        def load_sheet(sheet):
            raw = keep.tile([P, 2 * K], BF16, name="patch_raw%d" % sheet)
            src = patch_rows[SHEET * sheet : SHEET * (sheet + 1), :]
            nc.sync.dma_start(out=raw[:], in_=src.rearrange("(p n) k -> p (n k)", n=2))
            patch_raw[sheet] = raw

        def load_weight(h, groups):
            w = w_text if h == TEXT else w_patch[K_PASS * h : K_PASS * (h + 1), :]
            first, width = K_PASS * groups[0], K_PASS * len(groups)
            raw = keep.tile([P, PACK, width], BF16, name="weight_raw%d_%d" % (groups[0], h))
            nc.sync.dma_start(out=raw[:], in_=w[:, first : first + width].rearrange("(p j) c -> p j c", j=PACK))
            for n, g in enumerate(groups):
                weight_raw[g, h] = raw[:, :, K_PASS * n : K_PASS * (n + 1)]

        def load_per_image(name, src):
            sb = keep.tile([P, GROUPS, PACK * B], BF16, name=name)
            nc.sync.dma_start(out=sb[:], in_=src.rearrange("(g p t) b -> p g (t b)", p=P, t=PACK))
            return sb

        load_weight(0, [0])
        load_sheet(0)
        load_weight(0, [1])
        text_raw = keep.tile([P, KT], BF16, name="text_raw")
        nc.sync.dma_start(out=text_raw[:], in_=text)
        load_weight(TEXT, [0, 1])
        load_sheet(1)
        load_weight(1, [0, 1])
        shift_sb = load_per_image("shift_sb", shift)
        scale_sb = load_per_image("scale_sb", scale)
        for sheet in range(2, SHEETS):
            load_sheet(sheet)

        def quantize(codes, scales, values):
            nc.vector.quantize_mx(out=codes.bitcast(FP8X4), scales=scales, in_=values)

        def turn(word_rows, sorted_words):
            bank = psum.tile([P, len(word_rows) * 2 * P], F32, name="turn", bufs=2)
            for n, words in enumerate(word_rows):
                for u in range(2):
                    col = (2 * n + u) * P
                    nc.tensor.transpose(bank[:, col : col + P], words[:, u : 2 * P : 2], ident[:])
            nc.scalar.copy(
                out=sorted_words.rearrange("p (r w) -> p r w", r=P),
                in_=bank[:].rearrange("p (w r) -> p r w", r=P),
            )

        patch_codes = keep.tile([P, M // BANK, PASSES, BANK], U32, name="patch_codes", align_bytes=64)
        patch_scales = keep.tile([P, M // BANK, PASSES, BANK], U8, name="patch_scales", align_bytes=64)
        patch_sorted = {}

        def turn_sheet(sheet):
            words = patch_raw[sheet][:].bitcast(F32).rearrange("p (n h w) -> p n h w", n=2, h=PASSES)
            for h in range(PASSES):
                dst = stage.tile([P, 2 * SHEET], F32, name="patch_sorted", bufs=4 * PASSES, align_bytes=64)
                turn([words[:, n, h, :] for n in range(2)], dst[:])
                patch_sorted[sheet, h] = dst

        def patch_operand(first_sheet, sheets, h):
            c, at = divmod(SHEET * first_sheet, BANK)
            cols = slice(at, at + SHEET * sheets)
            return patch_codes[:, c, h, cols], patch_scales[:, c, h, cols]

        def quantize_sheet(sheet):
            for h in range(PASSES):
                codes, scales = patch_operand(sheet, 1, h)
                quantize(codes, scales, patch_sorted[sheet, h][:].bitcast(BF16))

        text_sorted = keep.tile([P, 2 * B], F32, name="text_sorted", align_bytes=64)
        text_codes = keep.tile([P, B], U32, name="text_codes", align_bytes=64)
        text_scales = keep.tile([P, B], U8, name="text_scales", align_bytes=64)

        weight_sorted, weight_codes, weight_scales = {}, {}, {}

        def sort_views(g, h, slots):
            if (g, h) not in weight_sorted:
                weight_sorted[g, h] = keep.tile(
                    [P, PACK, K_PASS], BF16, name="weight_sorted%d_%d" % (g, h), align_bytes=64
                )
            dst = weight_sorted[g, h][:].rearrange("p t (a i j) -> p a t i j", i=2, j=PACK)
            src = weight_raw[g, h].rearrange("p j (a i t) -> p a t i j", i=2, t=PACK)
            return dst[:, :, slots], src[:, :, slots]

        def sort_on_vector(g, h):
            dst, src = sort_views(g, h, slice(0, VECTOR_SLOTS[g, h]))
            nc.vector.tensor_copy(out=dst, in_=src)

        def sort_on_scalar(g, h):
            dst, src = sort_views(g, h, slice(VECTOR_SLOTS[g, h], PACK))
            nc.scalar.copy(out=dst, in_=src)

        def quantize_weight(g, h):
            codes = keep.tile([P, K_PASS], U32, name="weight_codes%d_%d" % (g, h), align_bytes=64)
            scales = keep.tile([P, K_PASS], U8, name="weight_scales%d_%d" % (g, h), align_bytes=64)
            quantize(codes[:], scales[:], weight_sorted[g, h][:].rearrange("p t c -> p (t c)"))
            weight_codes[g, h], weight_scales[g, h] = codes, scales

        def mx_pass(out, g, h, t, codes, scales, start, stop):
            cols = slice(P * t, P * (t + 1))
            nc.tensor.matmul_mx(
                out=out,
                lhsT=weight_codes[g, h][:, cols].bitcast(FP8X4),
                lhsT_scale=weight_scales[g, h][:, cols],
                rhs=codes.bitcast(FP8X4),
                rhs_scale=scales,
                start=start,
                stop=stop,
            )

        def slot_bank(t, width):
            return psum.tile([P, width], F32, name="slot%d" % t)

        text_bank, offset_sb, offset_turned, offset_ps = {}, {}, {}, {}

        def project_text(g):
            bank = slot_bank(PACK - GROUPS + g, PACK * B)
            for t in range(PACK):
                mx_pass(bank[:, B * t : B * (t + 1)], g, TEXT, t, text_codes[:], text_scales[:], True, True)
            text_bank[g] = bank

        def add_shift(g):
            sb = keep.tile([P, PACK * B], F32, name="offset_sb%d" % g)
            nc.vector.tensor_tensor(out=sb[:], in0=text_bank[g][:], in1=shift_sb[:, g, :], op=ALU.add)
            offset_sb[g] = sb

        def transpose_slots(bank, src):
            for t in range(PACK):
                nc.tensor.transpose(bank[:, P * t : P * (t + 1)], src[:, P * t : P * (t + 1)], ident[:])

        def offset_out(g):
            bank = psum.tile([P, PACK * P], F32, name="turn", bufs=2)
            transpose_slots(bank, offset_sb[g])
            sb = keep.tile([P, PACK * P], F32, name="offset_turned%d" % g)
            nc.scalar.copy(out=sb[:], in_=bank[:])
            offset_turned[g] = sb

        def offset_back(g):
            bank = psum.tile([P, PACK * B], F32, name="offset_ps%d" % g)
            transpose_slots(bank, offset_turned[g])
            offset_ps[g] = bank

        banks, y_sb, y_bf, fused_of = {}, {}, {}, {}

        def columns(unit):
            return slice(SHEET * unit[1], SHEET * (unit[1] + unit[2]))

        def images_of(unit):
            return SHEET * unit[2] // T

        def multiply(unit, t, passes):
            g, first_sheet, sheets = unit
            for h in passes:
                if h == 0:
                    banks[unit, t] = slot_bank(t, SHEET * sheets)
                codes, scales = patch_operand(first_sheet, sheets, h)
                mx_pass(banks[unit, t][:], g, h, t, codes, scales, h == 0, h == PASSES - 1)

        def image_column(unit, t, b):
            return B * t + SHEET * unit[1] // T + b

        def per_image(values, unit, t, lo, hi):
            cols = values[:, image_column(unit, t, lo) : image_column(unit, t, hi)]
            return cols.unsqueeze(2).to_broadcast([P, hi - lo, T])

        def by_image(tile_row, lo, hi):
            return tile_row[:, T * lo : T * hi].rearrange("p (b j) -> p b j", j=T)

        def pool_images(unit, t):
            left = fused_of[unit][2] or LEFT_IN_SLOT_2[unit[2]]
            return {0: images_of(unit), 2: images_of(unit) - left}.get(t, 0)

        def vector_images(unit, t):
            return images_of(unit) - (fused_of[unit][t] if t < LAST_SLOT else 0)

        def scale_slot(unit, t, following):
            g, y_t, bank = unit[0], y_sb[unit][:, t, :], banks[unit, t][:]
            hi, share = vector_images(unit, t), pool_images(unit, t)
            nc.vector.scalar_tensor_tensor(
                out=by_image(y_t, 0, hi),
                in0=per_image(scale_sb[:, g, :], unit, t, 0, hi),
                scalar=1.0,
                in1=by_image(bank, 0, hi),
                op0=ALU.add,
                op1=ALU.mult,
            )
            for b in range(hi, images_of(unit)):
                col = image_column(unit, t, b)
                nc.scalar.activation(
                    out=y_t[:, T * b : T * (b + 1)],
                    in_=bank[:, T * b : T * (b + 1)],
                    func=IDENTITY,
                    scale=gain[:, g, col : col + 1],
                    bias=offset_sb[g][:, col : col + 1],
                )
            if share > 0:
                part = by_image(y_t, 0, share)
                nc.gpsimd.tensor_tensor(
                    out=part, in0=part, in1=per_image(offset_sb[g][:], unit, t, 0, share), op=ALU.add
                )
            if following is not None:
                multiply(following, t, range(PASSES))

        def offset_slot(unit, t):
            lo, hi = pool_images(unit, t), vector_images(unit, t)
            if lo < hi:
                part = by_image(y_sb[unit][:, t, :], lo, hi)
                nc.vector.tensor_tensor(
                    out=part, in0=part, in1=per_image(offset_ps[unit[0]][:], unit, t, lo, hi), op=ALU.add
                )

        def store_y(unit, t0, t1):
            dst = y_out[K_PASS * unit[0] : K_PASS * (unit[0] + 1), columns(unit)]
            nc.sync.dma_start(
                out=dst.rearrange("(p t) m -> p t m", t=PACK)[:, t0:t1, :], in_=y_sb[unit][:, t0:t1, :]
            )

        def rounding_views(unit):
            rounded = stage.tile([P, SHEET * unit[2] * PACK], BF16, name="y_bf", bufs=4, align_bytes=64)
            y_bf[unit] = rounded
            dst = rounded[:].rearrange("p (a i t) -> p a t i", i=2, t=PACK)
            return dst, y_sb[unit][:].rearrange("p t (a i) -> p a t i", i=2)

        y_scales = keep.tile([P, M], U8, name="y_scales", align_bytes=64)

        def quantize_y(unit):
            g, cols = unit[0], columns(unit)
            codes = stage.tile([P, SHEET * unit[2]], U32, name="y_codes", bufs=4, align_bytes=64)
            quantize(codes[:], y_scales[SCALE_ROWS * g :, cols], y_bf[unit][:])
            nc.sync.dma_start(out=words_out[g, :, cols], in_=codes[:].bitcast(I32))


        units = [(g, first, 2) for first in range(0, SHEETS, 2) for g in range(GROUPS)]
        units = units[:-1] + [(GROUPS - 1, SHEETS - 2, 1), (GROUPS - 1, SHEETS - 1, 1)]

        sort_on_vector(0, 0)
        first_dst, first_src = sort_views(0, 0, slice(VECTOR_SLOTS[0, 0], PACK))
        nc.scalar.activation(out=first_dst, in_=first_src, func=IDENTITY)
        quantize_weight(0, 0)
        sort_on_vector(1, 0)
        sort_on_scalar(1, 0)
        turn_sheet(0)
        turn([text_raw[:].bitcast(F32)], text_sorted[:])
        quantize_weight(1, 0)
        quantize_sheet(0)
        quantize(text_codes[:], text_scales[:], text_sorted[:].bitcast(BF16))
        for g in range(GROUPS):
            sort_on_vector(g, TEXT)
            sort_on_scalar(g, TEXT)
        turn_sheet(1)
        for g in range(GROUPS):
            quantize_weight(g, TEXT)
            project_text(g)
        quantize_sheet(1)
        for g in range(GROUPS):
            sort_on_scalar(g, 1)
        sort_on_vector(0, 1)
        add_shift(0)
        for t in range(LAST_SLOT):
            multiply(units[0], t, [0])
        offset_out(0)
        quantize_weight(0, 1)
        sort_on_vector(1, 1)
        add_shift(1)
        for t in range(LAST_SLOT):
            multiply(units[0], t, [1])
        multiply(units[0], LAST_SLOT, range(PASSES))
        offset_back(0)
        gain = keep.tile([P, GROUPS, PACK * B], F32, name="gain")
        nc.scalar.activation(out=gain[:], in_=scale_sb[:], func=IDENTITY, bias=1.0)
        quantize_weight(1, 1)
        turn_sheet(2)

        last_step = len(units) - 1
        for s, unit in enumerate(units):
            following = units[s + 1] if s < last_step else None
            turning = s + 4 < SHEETS
            fused_of[unit] = FUSED if unit[2] == 2 and not turning else NOT_FUSED
            y_sb[unit] = stage.tile([P, PACK, SHEET * unit[2]], F32, name="y", bufs=6)
            for t in range(LAST_SLOT):
                scale_slot(unit, t, following)
                if s == 0 and t == 0:
                    turn_sheet(3)
            if s == 0:
                offset_out(1)
            else:
                offset_slot(units[s - 1], LAST_SLOT)
                store_y(units[s - 1], LAST_SLOT, PACK)
                dst, src = rounding_views(units[s - 1])
                nc.scalar.copy(out=dst, in_=src)
                if turning:
                    turn_sheet(s + 4)
            if s < last_step:
                for t in range(LAST_SLOT):
                    offset_slot(unit, t)
                scale_slot(unit, LAST_SLOT, following)
                store_y(unit, 0, LAST_SLOT)
            else:
                scale_slot(unit, LAST_SLOT, None)
                for t in range(PACK):
                    offset_slot(unit, t)
                store_y(unit, 0, PACK // 2)
                store_y(unit, PACK // 2, PACK)
            if s == 0:
                quantize_sheet(2)
            if s + 3 < SHEETS:
                quantize_sheet(s + 3)
            if s == 0:
                offset_back(1)
                turn_sheet(4)
            if s >= 2:
                quantize_y(units[s - 2])

        dst, src = rounding_views(units[last_step])
        nc.vector.tensor_copy(out=dst, in_=src)
        quantize_y(units[last_step - 1])
        quantize_y(units[last_step])
        for quadrant in range(P // 32):
            rows = slice(SCALE_ROWS * quadrant, SCALE_ROWS * (quadrant + 1))
            live = y_scales[32 * quadrant : 32 * quadrant + SCALE_ROWS * GROUPS, :]
            queue = nc.scalar if quadrant % 2 else nc.sync
            queue.dma_start(out=scales_out[:, rows, :], in_=live.bitcast(I32))
